import numpy as np
import ml_dtypes


def mxq(x, axis, fmt="e4m3"):
    dtype, down = {"e4m3": (ml_dtypes.float8_e4m3fn, 7), "e5m2": (ml_dtypes.float8_e5m2, 14)}[fmt]
    v = np.moveaxis(np.asarray(x, np.float32).astype(ml_dtypes.bfloat16).astype(np.float64), axis, -1)
    blocks = v.reshape(v.shape[:-1] + (-1, 32))
    amax = np.abs(blocks).max(-1, keepdims=True)
    byte = np.maximum(np.where(amax > 0, np.frexp(amax)[1] - 1 + 127, 0) - down, 1)
    scale = np.exp2(byte - 127.0)
    codes = (blocks / scale).astype(np.float32).astype(dtype).astype(np.float64)
    return np.moveaxis((codes * scale).reshape(v.shape), -1, axis)


WIDE = False


def mx_kscale(k):
    if not WIDE:
        return np.ones(k)
    levels = np.array([10, -10, 5, -5, 0])
    if k % 512:
        return np.exp2(np.random.permutation(np.resize(levels, k // 32))).repeat(32)
    a = np.empty((k // 512, 16))
    for p in range(k // 512):
        a[p, :8] = np.random.permutation(np.resize(levels, 8))
        for g in range(8):
            far = levels[np.abs(levels - a[p, g]) >= 10]
            a[p, g + 8] = far[np.random.randint(len(far))]
    return np.exp2(a.ravel()).repeat(32)


def f64(x):
    return np.asarray(x).astype(np.float64)


def striped(idx):
    return np.tile(np.asarray(idx).reshape(-1, 16).T, (8, 1)).astype(np.uint16)


def unstriped(offs):
    return offs[:16].T.reshape(-1).astype(np.int64)


E2M1 = np.array([0.0, 0.5, 1.0, 1.5, 2.0, 3.0, 4.0, 6.0, -0.0, -0.5, -1.0, -1.5, -2.0, -3.0, -4.0, -6.0])


def pack_weight(w, fmt):
    k, n = w.shape
    w = f64(np.asarray(w, np.float32).astype(ml_dtypes.bfloat16)).reshape(k // 32, 32, n)
    amax = np.abs(w).max(1)
    if fmt == "e4m3":
        byte = np.frexp(amax)[1] - 1 + 127 - 7
    else:
        mant, ex = np.frexp(amax / 6.0)
        byte = np.where(mant > 0.5, ex, ex - 1) + 127
    byte = np.clip(np.where(amax > 0, byte, 1), 1, 254)
    scaled = (w * np.exp2(127.0 - byte)[:, None, :]).reshape(k, n).astype(np.float32)
    by_word = np.ascontiguousarray(scaled.reshape(k // 512, 128, 4, n).transpose(0, 1, 3, 2))
    if fmt == "e4m3":
        words = by_word.astype(ml_dtypes.float8_e4m3fn).view(np.uint8)
    else:
        c = by_word.astype(ml_dtypes.float4_e2m1fn).view(np.uint8) & 0xF
        words = (c[..., 0::2] | (c[..., 1::2] << 4)).reshape(k // 512, 128, 2 * n)
    return np.ascontiguousarray(words), np.ascontiguousarray(byte.astype(np.uint8).reshape(k // 512, 16, n))


def unpack_weight(words, scales, fmt):
    g, _, n = scales.shape
    words = np.ascontiguousarray(words).reshape(g, 128, n, -1)
    if fmt == "e4m3":
        vals = words.view(ml_dtypes.float8_e4m3fn).astype(np.float64)
    else:
        nib = np.empty((g, 128, n, 4), np.uint8)
        nib[..., 0::2] = words & 0xF
        nib[..., 1::2] = words >> 4
        vals = E2M1[nib]
    vals = vals * np.repeat(np.exp2(scales.astype(np.float64) - 127.0), 8, axis=1)[..., None]
    return vals.transpose(0, 1, 3, 2).reshape(g * 512, n)


B, N, T, D, DV, NQ = 1, 1536, 4096, 512, 128, 256
PAGE = 512


def setup_inputs():
    n = np.random.standard_normal
    pages = np.random.permutation(T // PAGE)[:B * N // PAGE]
    idx = (pages[:, None] * PAGE + np.arange(PAGE)[None, :]).reshape(-1)
    s = mx_kscale(D)[:, None]
    u = np.ones(T)
    u[idx] = mx_kscale(B * N)
    r = np.random.uniform(0.5, 2.0, T)
    k = n((D, T)) / s
    v = n((DV, T)) / (u * r)
    kp = pack_weight(k, "e4m3")
    vp = pack_weight(v.T, "e4m3")
    return {
        "qT": (n((B, D, NQ)) * s * (1.00 / np.sqrt(D))).astype(np.float32),
        "k_words": kp[0],
        "k_scales": kp[1],
        "v_words": vp[0],
        "v_scales": vp[1],
        "vs": np.tile(u * r, (128, 1)).astype(np.float32),
        "kb": np.tile(n(T), (128, 1)).astype(np.float32),
        "sink": (2.0 + 3.0 * n((B, NQ, 1))).astype(np.float32),
        "offs": striped(idx),
        "voffs": striped((pages[:, None] * DV + np.arange(DV)[None, :]).reshape(-1)),
    }


def reference(qT, k_words, k_scales, v_words, v_scales, vs, kb, sink, offs, voffs):
    idx = unstriped(offs)
    k = unpack_weight(k_words, k_scales, "e4m3")
    v = unpack_weight(v_words, v_scales, "e4m3")
    v = v.reshape(T // 512, 512, DV)[unstriped(voffs)[::DV] // DV].reshape(B, N, DV)
    pick = lambda x: x[:, idx].reshape(x.shape[0], B, N).transpose(1, 0, 2)
    q = f64(qT)
    score = mxq(q, 1, "e4m3").transpose(0, 2, 1) @ pick(k)
    score = score + pick(f64(kb))[:, :1, :]
    m = np.maximum(score.max(-1, keepdims=True), f64(sink))
    p = np.exp(score - m)
    total = p.sum(-1, keepdims=True) + np.exp(f64(sink) - m)
    w = p * pick(f64(vs))[:, :1, :]
    y = mxq(w, 2, "e4m3") @ v
    y = y / total
    return y

@@ -1,0 +1,237 @@
+from contextlib import ExitStack
+
+import concourse.mybir as mybir
+from concourse.masks import make_identity
+
+F32 = mybir.dt.float32
+BF16 = mybir.dt.bfloat16
+I32 = mybir.dt.int32
+U32 = mybir.dt.uint32
+U16 = mybir.dt.uint16
+U8 = mybir.dt.uint8
+FP8X4 = mybir.dt.float8_e4m3fn_x4
+ALU = mybir.AluOpType
+ACT = mybir.ActivationFunctionType
+AX = mybir.AxisListType
+
+P = 128
+PACK = 4
+NQ, N, T, D, DV = 256, 1536, 4096, 512, 128
+PAGE = 512
+PAGES = N // PAGE
+HALVES = NQ // P
+LIVE = P - 1
+FLOPS = 2 * NQ * N * (D + DV)
+
+
+def tile_attend_pkv8_soft_sink_kb_kernel(
+    tc, qT, k_words, k_scales, v_words, v_scales, vs, kb, sink, offs, voffs, out
+):
+    nc = tc.nc
+    with ExitStack() as ctx:
+        sb = ctx.enter_context(tc.tile_pool(name="sb", bufs=1))
+        ps = ctx.enter_context(tc.psum_pool(name="ps", bufs=1))
+
+        offs_t = sb.tile([P, N // 16], U16, name="offs_t")
+        voffs_t = sb.tile([P, PAGES * DV // 16], U16, name="voffs_t")
+        kw_pool = sb.tile([P, T], I32, name="kw_pool")
+        ks_pool = sb.tile([P, T], U8, name="ks_pool")
+        vw_pool = sb.tile([P, T // PAGE * DV], I32, name="vw_pool")
+        vsc_pool = sb.tile([P, T // PAGE * DV], U8, name="vsc_pool")
+        kb_pool = sb.tile([P, T], F32, name="kb_pool")
+        vs_pool = sb.tile([P, T], F32, name="vs_pool")
+        q_raw = sb.tile([P, PACK, NQ], F32, name="q_raw")
+        sink_t = sb.tile([P, HALVES], F32, name="sink_t")
+        ident = sb.tile([P, P], F32, name="ident")
+        warm = sb.tile([P, 1], F32, name="warm")
+
+        q_bf = sb.tile([P, HALVES, P, PACK], BF16, name="q_bf", align_bytes=64)
+        q_codes = sb.tile([P, NQ], U32, name="q_codes", align_bytes=64)
+        q_sc = sb.tile([P, NQ], U8, name="q_sc", align_bytes=64)
+        kw = sb.tile([P, N], U32, name="kw", align_bytes=64)
+        ks = sb.tile([P, N], U8, name="ks", align_bytes=64)
+        vw = sb.tile([P, PAGES * DV], U32, name="vw", align_bytes=64)
+        vsc = sb.tile([P, PAGES * DV], U8, name="vsc", align_bytes=64)
+        kb_row = sb.tile([P, N], F32, name="kb_row")
+        vs_row = sb.tile([P, N], F32, name="vs_row")
+        kb_col = sb.tile([P, PAGES, PACK], F32, name="kb_col")
+        vs_col = sb.tile([P, PAGES, PACK], F32, name="vs_col")
+        s_turned = sb.tile([P, HALVES, PAGES, PACK, P], F32, name="s_turned")
+        neg_s = sb.tile([P, HALVES, PAGES, PAGE], F32, name="neg_s")
+        prob = sb.tile([P, HALVES, PAGES, PAGE], F32, name="prob")
+        w_bf = sb.tile([P, HALVES, PAGES, P, PACK], BF16, name="w_bf", align_bytes=64)
+        w_codes = sb.tile([P, HALVES, PAGES, P], U32, name="w_codes", align_bytes=64)
+        w_sc = sb.tile([P, HALVES, PAGES, P], U8, name="w_sc", align_bytes=64)
+        mins = sb.tile([P, HALVES, PAGES + 1], F32, name="mins")
+        neg_m = sb.tile([P, HALVES], F32, name="neg_m")
+        sums = sb.tile([P, HALVES, PAGES + 1], F32, name="sums")
+        total = sb.tile([P, HALVES], F32, name="total")
+        inv = sb.tile([P, HALVES], F32, name="inv")
+        y_sb = sb.tile([P, HALVES, DV], F32, name="y_sb")
+
+        def page_offs(g):
+            return offs_t[:, g * PAGE // 16 : (g + 1) * PAGE // 16]
+
+        def page_cols(g):
+            return slice(g * PAGE, (g + 1) * PAGE)
+
+        nc.vector.memset(ks_pool[:].bitcast(I32), 0)
+        nc.vector.memset(warm[:], 0.0)
+        nc.vector.memset(kb_pool[0:LIVE, :], 0.0)
+        nc.vector.memset(vsc_pool[:].bitcast(I32), 0)
+        nc.vector.memset(vs_pool[0:LIVE, 0:32], 0.0)
+        nc.scalar.activation(warm[:], warm[:], ACT.Exp)
+        make_identity(nc, ident[:])
+        for a in range(4):
+            nc.gpsimd.memset(vs_pool[0:LIVE, max(16, a * 1024) : (a + 1) * 1024], 0.0)
+
+        nc.sync.dma_start(offs_t[:], offs)
+        nc.sync.dma_start(q_raw[:], qT[0].rearrange("(p j) q -> p j q", j=PACK))
+        nc.sync.dma_start(kb_pool[LIVE:P, :], kb[0:1, :])
+        for a in range(4):
+            nc.sync.dma_start(
+                ks_pool[32 * a : 32 * a + 4, :].bitcast(I32), k_scales[0, 4 * a : 4 * a + 4, :].bitcast(I32)
+            )
+        nc.sync.dma_start(kw_pool[:], k_words[0].rearrange("p t r -> p (t r)").bitcast(I32))
+        nc.sync.dma_start(vs_pool[LIVE:P, :], vs[0:1, :])
+        nc.sync.dma_start(sink_t[:], sink[0].rearrange("(p c) o -> p (c o)", c=HALVES))
+        nc.sync.dma_start(voffs_t[:], voffs)
+        nc.sync.dma_start(
+            vw_pool[:].rearrange("p (u e) -> p u e", e=DV),
+            v_words.rearrange("u p e r -> p u (e r)").bitcast(I32),
+        )
+        for a in range(4):
+            nc.sync.dma_start(
+                vsc_pool[32 * a : 32 * a + 4, :].bitcast(I32).rearrange("f (u e) -> f u e", e=DV // 4),
+                v_scales[:, 4 * a : 4 * a + 4, :].rearrange("u f e -> f u e").bitcast(I32),
+            )
+
+        q_view = q_raw[:].rearrange("p j (m c) -> p c m j", c=HALVES)
+        for c in range(HALVES):
+            nc.scalar.copy(q_bf[:, c], q_view[:, c])
+
+        for g in range(PAGES):
+            nc.vector.tensor_copy(kb_row[:, page_cols(g)], kb_pool[:].indirect(page_offs(g)))
+            bank = ps.tile([P, PACK, P], F32, name="turn2", tag="turn2", bufs=2)
+            for j in range(PACK):
+                lo = g * PAGE + j * P
+                nc.tensor.transpose(bank[:, j, :], kb_row[:, lo : lo + P], ident[:])
+            nc.scalar.copy(kb_col[:, g, :], bank[:, :, LIVE])
+        for g in range(PAGES):
+            nc.vector.tensor_copy(ks[:, page_cols(g)], ks_pool[:].indirect(page_offs(g)))
+        nc.vector.quantize_mx(
+            out=q_codes[:].bitcast(FP8X4), scales=q_sc[:], in_=q_bf[:].rearrange("p c m j -> p (c m j)")
+        )
+        nc.vector.tensor_scalar(mins[:, :, PAGES], sink_t[:], -1.0, None, ALU.mult)
+        for g in range(PAGES):
+            nc.vector.tensor_copy(kw[:, page_cols(g)], kw_pool[:].bitcast(U32).indirect(page_offs(g)))
+
+        def scores(c, g):
+            bank = ps.tile([P, PACK, P], F32, name="score", tag="score", bufs=2)
+            for j in range(PACK):
+                cols = slice(g * PAGE + j * P, g * PAGE + (j + 1) * P)
+                nc.tensor.matmul_mx(
+                    out=bank[:, j, :],
+                    lhsT=kw[:, cols].bitcast(FP8X4),
+                    lhsT_scale=ks[:, cols],
+                    rhs=q_codes[:, c * P : (c + 1) * P].bitcast(FP8X4),
+                    rhs_scale=q_sc[:, c * P : (c + 1) * P],
+                    start=True,
+                    stop=True,
+                )
+            for j in range(PACK):
+                nc.scalar.activation(
+                    s_turned[:, c, g, j, :], bank[:, j, :], ACT.Identity, bias=kb_col[:, g, j : j + 1]
+                )
+
+        def turn_and_min(c, g):
+            bank = ps.tile([P, PAGE], F32, name="turn1", tag="turn1", bufs=2)
+            for j in range(PACK):
+                nc.tensor.transpose(bank[:, j * P : (j + 1) * P], s_turned[:, c, g, j, :], ident[:])
+            nc.vector.tensor_scalar(
+                neg_s[:, c, g, :].rearrange("q (t s) -> q t s", t=PACK),
+                bank[:].rearrange("q (s t) -> q t s", t=PACK),
+                -1.0,
+                None,
+                ALU.mult,
+                ALU.min,
+                accum_out=mins[:, c, g : g + 1],
+            )
+            if g == PAGES - 1:
+                nc.vector.tensor_reduce(neg_m[:, c : c + 1], mins[:, c, :], AX.X, ALU.min)
+
+        steps = [(c, g) for c in range(HALVES) for g in range(PAGES)]
+        for i in range(len(steps) + 1):
+            if i < len(steps):
+                scores(*steps[i])
+            if i >= 1:
+                turn_and_min(*steps[i - 1])
+
+        for g in range(PAGES):
+            nc.vector.tensor_copy(vs_row[:, page_cols(g)], vs_pool[:].indirect(page_offs(g)))
+            bank = ps.tile([P, PACK, P], F32, name="turn2", tag="turn2", bufs=2)
+            for t in range(PACK):
+                nc.tensor.transpose(bank[:, t, :], vs_row[:, g * PAGE + t : (g + 1) * PAGE : PACK], ident[:])
+            nc.scalar.copy(vs_col[:, g, :], bank[:, :, LIVE])
+        nc.vector.tensor_copy(vw[:], vw_pool[:].bitcast(U32).indirect(voffs_t[:]))
+        nc.vector.tensor_copy(vsc[:], vsc_pool[:].indirect(voffs_t[:]))
+
+        y_banks = [ps.tile([P, DV], F32, name=f"y{c}", tag=f"y{c}") for c in range(HALVES)]
+
+        def weigh(c, g):
+            nc.scalar.activation(
+                prob[:, c, g, :],
+                neg_s[:, c, g, :],
+                ACT.Exp,
+                bias=neg_m[:, c : c + 1],
+                scale=-1.0,
+                accum_out=sums[:, c, g : g + 1],
+            )
+            if g == PAGES - 1:
+                nc.scalar.activation(
+                    sums[:, c, PAGES : PAGES + 1],
+                    mins[:, c, PAGES : PAGES + 1],
+                    ACT.Exp,
+                    bias=neg_m[:, c : c + 1],
+                    scale=-1.0,
+                )
+            bank = ps.tile([P, PACK, P], F32, name="turn2", tag="turn2", bufs=2)
+            for t in range(PACK):
+                nc.tensor.transpose(bank[:, t, :], prob[:, c, g, t * P : (t + 1) * P], ident[:])
+            nc.vector.tensor_tensor(
+                w_bf[:, c, g],
+                bank[:].rearrange("p t q -> p q t"),
+                vs_col[:, g, :].unsqueeze(1).to_broadcast([P, P, PACK]),
+                ALU.mult,
+            )
+
+        def multiply(c, g):
+            nc.vector.quantize_mx(
+                out=w_codes[:, c, g, :].bitcast(FP8X4),
+                scales=w_sc[:, c, g, :],
+                in_=w_bf[:, c, g].rearrange("p q t -> p (q t)"),
+            )
+            nc.tensor.matmul_mx(
+                out=y_banks[c][:],
+                lhsT=w_codes[:, c, g, :].bitcast(FP8X4),
+                lhsT_scale=w_sc[:, c, g, :],
+                rhs=vw[:, g * DV : (g + 1) * DV].bitcast(FP8X4),
+                rhs_scale=vsc[:, g * DV : (g + 1) * DV],
+                start=(g == 0),
+                stop=(g == PAGES - 1),
+            )
+
+        for i in range(len(steps) + 1):
+            if i < len(steps):
+                weigh(*steps[i])
+            if i == len(steps) - 1:
+                nc.vector.tensor_reduce(total[:], sums[:], AX.X, ALU.add)
+            if i >= 1:
+                multiply(*steps[i - 1])
+            if i == len(steps) - 1:
+                nc.vector.reciprocal(inv[:], total[:])
+
+        out_view = out[0].rearrange("(p c) e -> p c e", c=HALVES)
+        for c in range(HALVES):
+            nc.scalar.activation(y_sb[:, c, :], y_banks[c][:], ACT.Copy, scale=inv[:, c : c + 1])
+            nc.sync.dma_start(out_view[:, c, :], y_sb[:, c, :])

@@ -36,16 +36,16 @@ def tile_attend_pkv8_soft_sink_kb_kernel(
         voffs_t = sb.tile([P, PAGES * DV // 16], U16, name="voffs_t")
         kw_pool = sb.tile([P, T], I32, name="kw_pool")
         ks_pool = sb.tile([P, T], U8, name="ks_pool")
-        vw_pool = sb.tile([P, T // PAGE * DV], I32, name="vw_pool")
         vsc_pool = sb.tile([P, T // PAGE * DV], U8, name="vsc_pool")
         kb_pool = sb.tile([P, T], F32, name="kb_pool")
-        vs_pool = sb.tile([P, T], F32, name="vs_pool")
+        zero = sb.tile([P, 1], F32, name="zero")
         q_raw = sb.tile([P, PACK, NQ], F32, name="q_raw")
+        vs_pool = sb.tile([P, T], F32, name="vs_pool")
         sink_t = sb.tile([P, HALVES], F32, name="sink_t")
         ident = sb.tile([P, P], F32, name="ident")
         warm = sb.tile([P, 1], F32, name="warm")
 
-        q_bf = sb.tile([P, HALVES, P, PACK], BF16, name="q_bf", align_bytes=64)
+        q_bf = sb.tile([P, HALVES, P, PACK], BF16, name="q_bf", tag="q_bf_then_vw", align_bytes=64)
         q_codes = sb.tile([P, NQ], U32, name="q_codes", align_bytes=64)
         q_sc = sb.tile([P, NQ], U8, name="q_sc", align_bytes=64)
         kw = sb.tile([P, N], U32, name="kw", align_bytes=64)
@@ -54,16 +54,16 @@ def tile_attend_pkv8_soft_sink_kb_kernel(
         vsc = sb.tile([P, PAGES * DV], U8, name="vsc", align_bytes=64)
         kb_row = sb.tile([P, N], F32, name="kb_row")
         vs_row = sb.tile([P, N], F32, name="vs_row")
-        kb_col = sb.tile([P, PAGES, PACK], F32, name="kb_col")
-        vs_col = sb.tile([P, PAGES, PACK], F32, name="vs_col")
+        kb_col = [sb.tile([P, PACK], F32, name=f"kb_col{g}") for g in range(PAGES)]
+        vs_col = [sb.tile([P, PACK], F32, name=f"vs_col{g}") for g in range(PAGES)]
         s_turned = sb.tile([P, HALVES, PAGES, PACK, P], F32, name="s_turned")
         neg_s = sb.tile([P, HALVES, PAGES, PAGE], F32, name="neg_s")
         prob = sb.tile([P, HALVES, PAGES, PAGE], F32, name="prob")
-        w_bf = sb.tile([P, HALVES, PAGES, P, PACK], BF16, name="w_bf", align_bytes=64)
-        w_codes = sb.tile([P, HALVES, PAGES, P], U32, name="w_codes", align_bytes=64)
-        w_sc = sb.tile([P, HALVES, PAGES, P], U8, name="w_sc", align_bytes=64)
-        mins = sb.tile([P, HALVES, PAGES + 1], F32, name="mins")
-        neg_m = sb.tile([P, HALVES], F32, name="neg_m")
+        w_bf = sb.tile([P, HALVES * PAGES, P, PACK], BF16, name="w_bf", align_bytes=64)
+        w_codes = sb.tile([P, HALVES * PAGES, P], U32, name="w_codes", align_bytes=64)
+        w_sc = sb.tile([P, HALVES * PAGES, P], U8, name="w_sc", align_bytes=64)
+        mins = sb.tile([P, HALVES, PAGES], F32, name="mins")
+        neg_sink = sb.tile([P, HALVES], F32, name="neg_sink")
         sums = sb.tile([P, HALVES, PAGES + 1], F32, name="sums")
         total = sb.tile([P, HALVES], F32, name="total")
         inv = sb.tile([P, HALVES], F32, name="inv")
@@ -76,58 +76,66 @@ def tile_attend_pkv8_soft_sink_kb_kernel(
             return slice(g * PAGE, (g + 1) * PAGE)
 
         nc.vector.memset(ks_pool[:].bitcast(I32), 0)
-        nc.vector.memset(warm[:], 0.0)
+        nc.vector.memset(zero[:], 0.0)
         nc.vector.memset(kb_pool[0:LIVE, :], 0.0)
-        nc.vector.memset(vsc_pool[:].bitcast(I32), 0)
-        nc.vector.memset(vs_pool[0:LIVE, 0:32], 0.0)
-        nc.scalar.activation(warm[:], warm[:], ACT.Exp)
+        vs_pieces = vs_pool[0:LIVE, :].rearrange("p (a x) -> p a x", a=8)
+        nc.vector.memset(vs_pieces[:, :, 0:8], 0.0)
+        nc.scalar.activation(warm[:], zero[:], ACT.Exp)
         make_identity(nc, ident[:])
-        for a in range(4):
-            nc.gpsimd.memset(vs_pool[0:LIVE, max(16, a * 1024) : (a + 1) * 1024], 0.0)
+        for a in range(8):
+            nc.gpsimd.memset(vs_pieces[:, a, :], 0.0)
 
         nc.sync.dma_start(offs_t[:], offs)
-        nc.sync.dma_start(q_raw[:], qT[0].rearrange("(p j) q -> p j q", j=PACK))
         nc.sync.dma_start(kb_pool[LIVE:P, :], kb[0:1, :])
+        nc.sync.dma_start(q_raw[:], qT[0].rearrange("(p j) q -> p j q", j=PACK))
         for a in range(4):
-            nc.sync.dma_start(
+            nc.scalar.dma_start(
                 ks_pool[32 * a : 32 * a + 4, :].bitcast(I32), k_scales[0, 4 * a : 4 * a + 4, :].bitcast(I32)
             )
         nc.sync.dma_start(kw_pool[:], k_words[0].rearrange("p t r -> p (t r)").bitcast(I32))
         nc.sync.dma_start(vs_pool[LIVE:P, :], vs[0:1, :])
         nc.sync.dma_start(sink_t[:], sink[0].rearrange("(p c) o -> p (c o)", c=HALVES))
         nc.sync.dma_start(voffs_t[:], voffs)
+
+        q_view = q_raw[:].rearrange("p j (m c) -> p c m j", c=HALVES)
+        for c in range(HALVES):
+            nc.scalar.copy(q_bf[:, c], q_view[:, c])
+
+        def gather_kb(g):
+            nc.vector.tensor_copy(kb_row[:, page_cols(g)], kb_pool[:].indirect(page_offs(g)))
+            bank = ps.tile([P, PACK, P], F32, name="kb_bank", tag=f"bank{5 + g}")
+            for j in range(PACK):
+                lo = g * PAGE + j * P
+                nc.tensor.transpose(bank[:, j, :], kb_row[:, lo : lo + P], ident[:])
+            nc.scalar.copy(kb_col[g][:], bank[:, :, LIVE])
+
+        for g in range(PAGES):
+            gather_kb(g)
+        nc.vector.tensor_copy(ks[:], ks_pool[:].indirect(offs_t[:]))
+        nc.vector.quantize_mx(
+            out=q_codes[:].bitcast(FP8X4), scales=q_sc[:], in_=q_bf[:].rearrange("p c m j -> p (c m j)")
+        )
+        vw_pool = sb.tile([P, T // PAGE * DV], I32, name="vw_pool", tag="q_bf_then_vw", align_bytes=64)
         nc.sync.dma_start(
             vw_pool[:].rearrange("p (u e) -> p u e", e=DV),
             v_words.rearrange("u p e r -> p u (e r)").bitcast(I32),
         )
+        nc.vector.tensor_copy(kw[:], kw_pool[:].bitcast(U32).indirect(offs_t[:]))
+
+        nc.vector.memset(vsc_pool[:].bitcast(I32), 0)
         for a in range(4):
             nc.sync.dma_start(
                 vsc_pool[32 * a : 32 * a + 4, :].bitcast(I32).rearrange("f (u e) -> f u e", e=DV // 4),
                 v_scales[:, 4 * a : 4 * a + 4, :].rearrange("u f e -> f u e").bitcast(I32),
             )
 
-        q_view = q_raw[:].rearrange("p j (m c) -> p c m j", c=HALVES)
-        for c in range(HALVES):
-            nc.scalar.copy(q_bf[:, c], q_view[:, c])
+        nc.vector.tensor_scalar(neg_sink[:], sink_t[:], -1.0, None, ALU.mult)
 
-        for g in range(PAGES):
-            nc.vector.tensor_copy(kb_row[:, page_cols(g)], kb_pool[:].indirect(page_offs(g)))
-            bank = ps.tile([P, PACK, P], F32, name="turn2", tag="turn2", bufs=2)
-            for j in range(PACK):
-                lo = g * PAGE + j * P
-                nc.tensor.transpose(bank[:, j, :], kb_row[:, lo : lo + P], ident[:])
-            nc.scalar.copy(kb_col[:, g, :], bank[:, :, LIVE])
-        for g in range(PAGES):
-            nc.vector.tensor_copy(ks[:, page_cols(g)], ks_pool[:].indirect(page_offs(g)))
-        nc.vector.quantize_mx(
-            out=q_codes[:].bitcast(FP8X4), scales=q_sc[:], in_=q_bf[:].rearrange("p c m j -> p (c m j)")
-        )
-        nc.vector.tensor_scalar(mins[:, :, PAGES], sink_t[:], -1.0, None, ALU.mult)
-        for g in range(PAGES):
-            nc.vector.tensor_copy(kw[:, page_cols(g)], kw_pool[:].bitcast(U32).indirect(page_offs(g)))
+        steps = [(c, g) for c in range(HALVES) for g in range(PAGES)]
 
-        def scores(c, g):
-            bank = ps.tile([P, PACK, P], F32, name="score", tag="score", bufs=2)
+        def scores(i):
+            c, g = steps[i]
+            bank = ps.tile([P, PACK, P], F32, name="score", tag=f"bank{i}")
             for j in range(PACK):
                 cols = slice(g * PAGE + j * P, g * PAGE + (j + 1) * P)
                 nc.tensor.matmul_mx(
@@ -141,95 +149,91 @@ def tile_attend_pkv8_soft_sink_kb_kernel(
                 )
             for j in range(PACK):
                 nc.scalar.activation(
-                    s_turned[:, c, g, j, :], bank[:, j, :], ACT.Identity, bias=kb_col[:, g, j : j + 1]
+                    s_turned[:, c, g, j, :], bank[:, j, :], ACT.Identity, bias=kb_col[g][:, j : j + 1]
                 )
 
-        def turn_and_min(c, g):
-            bank = ps.tile([P, PAGE], F32, name="turn1", tag="turn1", bufs=2)
+        def turn_and_min(i):
+            c, g = steps[i]
+            bank = ps.tile([P, PAGE], F32, name="turn1", tag=f"bank{i}")
             for j in range(PACK):
                 nc.tensor.transpose(bank[:, j * P : (j + 1) * P], s_turned[:, c, g, j, :], ident[:])
             nc.vector.tensor_scalar(
                 neg_s[:, c, g, :].rearrange("q (t s) -> q t s", t=PACK),
                 bank[:].rearrange("q (s t) -> q t s", t=PACK),
                 -1.0,
-                None,
+                neg_sink[:, c : c + 1] if g == 0 else mins[:, c, g - 1 : g],
                 ALU.mult,
                 ALU.min,
                 accum_out=mins[:, c, g : g + 1],
             )
-            if g == PAGES - 1:
-                nc.vector.tensor_reduce(neg_m[:, c : c + 1], mins[:, c, :], AX.X, ALU.min)
 
-        steps = [(c, g) for c in range(HALVES) for g in range(PAGES)]
-        for i in range(len(steps) + 1):
-            if i < len(steps):
-                scores(*steps[i])
-            if i >= 1:
-                turn_and_min(*steps[i - 1])
+        for i in range(4):
+            scores(i)
+        for i in range(2):
+            turn_and_min(i)
+        for i in range(4, 6):
+            scores(i)
+        for i in range(2, 6):
+            turn_and_min(i)
 
         for g in range(PAGES):
             nc.vector.tensor_copy(vs_row[:, page_cols(g)], vs_pool[:].indirect(page_offs(g)))
-            bank = ps.tile([P, PACK, P], F32, name="turn2", tag="turn2", bufs=2)
-            for t in range(PACK):
-                nc.tensor.transpose(bank[:, t, :], vs_row[:, g * PAGE + t : (g + 1) * PAGE : PACK], ident[:])
-            nc.scalar.copy(vs_col[:, g, :], bank[:, :, LIVE])
+            nc.sync.dma_start(vs_col[g][:], vs_row[LIVE:P, page_cols(g)])
         nc.vector.tensor_copy(vw[:], vw_pool[:].bitcast(U32).indirect(voffs_t[:]))
         nc.vector.tensor_copy(vsc[:], vsc_pool[:].indirect(voffs_t[:]))
 
-        y_banks = [ps.tile([P, DV], F32, name=f"y{c}", tag=f"y{c}") for c in range(HALVES)]
-
-        def weigh(c, g):
-            nc.scalar.activation(
-                prob[:, c, g, :],
-                neg_s[:, c, g, :],
-                ACT.Exp,
-                bias=neg_m[:, c : c + 1],
-                scale=-1.0,
-                accum_out=sums[:, c, g : g + 1],
-            )
-            if g == PAGES - 1:
+        p_banks = {}
+        for c in range(HALVES):
+            neg_m = mins[:, c, PAGES - 1 : PAGES]
+            for g in range(PAGES):
                 nc.scalar.activation(
-                    sums[:, c, PAGES : PAGES + 1],
-                    mins[:, c, PAGES : PAGES + 1],
-                    ACT.Exp,
-                    bias=neg_m[:, c : c + 1],
-                    scale=-1.0,
+                    prob[:, c, g, :], neg_s[:, c, g, :], ACT.Exp, bias=neg_m, scale=-1.0,
+                    accum_out=sums[:, c, g : g + 1],
                 )
-            bank = ps.tile([P, PACK, P], F32, name="turn2", tag="turn2", bufs=2)
-            for t in range(PACK):
-                nc.tensor.transpose(bank[:, t, :], prob[:, c, g, t * P : (t + 1) * P], ident[:])
+                bank = ps.tile([P, PACK, P], F32, name="turn2", tag=f"bank{steps.index((c, g))}")
+                p_banks[c, g] = bank
+                for t in range(PACK):
+                    nc.tensor.transpose(bank[:, t, :], prob[:, c, g, t * P : (t + 1) * P], ident[:])
+            nc.scalar.activation(
+                sums[:, c, PAGES : PAGES + 1], neg_sink[:, c : c + 1], ACT.Exp, bias=neg_m, scale=-1.0
+            )
+        y_banks = [ps.tile([P, DV], F32, name=f"y{c}", tag=f"bank{6 + c}") for c in range(HALVES)]
+
+        w_order = steps
+
+        def weigh_on_vector(c, g):
             nc.vector.tensor_tensor(
-                w_bf[:, c, g],
-                bank[:].rearrange("p t q -> p q t"),
-                vs_col[:, g, :].unsqueeze(1).to_broadcast([P, P, PACK]),
+                w_bf[:, w_order.index((c, g))],
+                p_banks[c, g][:].rearrange("p t q -> p q t"),
+                vs_col[g][:].unsqueeze(1).to_broadcast([P, P, PACK]),
                 ALU.mult,
             )
 
-        def multiply(c, g):
+        def multiply(lo, hi):
             nc.vector.quantize_mx(
-                out=w_codes[:, c, g, :].bitcast(FP8X4),
-                scales=w_sc[:, c, g, :],
-                in_=w_bf[:, c, g].rearrange("p q t -> p (q t)"),
+                out=w_codes[:].rearrange("p i q -> p (i q)")[:, lo * P : hi * P].bitcast(FP8X4),
+                scales=w_sc[:].rearrange("p i q -> p (i q)")[:, lo * P : hi * P],
+                in_=w_bf[:].rearrange("p i q t -> p (i q t)")[:, lo * PAGE : hi * PAGE],
             )
-            nc.tensor.matmul_mx(
-                out=y_banks[c][:],
-                lhsT=w_codes[:, c, g, :].bitcast(FP8X4),
-                lhsT_scale=w_sc[:, c, g, :],
-                rhs=vw[:, g * DV : (g + 1) * DV].bitcast(FP8X4),
-                rhs_scale=vsc[:, g * DV : (g + 1) * DV],
-                start=(g == 0),
-                stop=(g == PAGES - 1),
-            )
+            for i in range(lo, hi):
+                c, g = w_order[i]
+                nc.tensor.matmul_mx(
+                    out=y_banks[c][:],
+                    lhsT=w_codes[:, i, :].bitcast(FP8X4),
+                    lhsT_scale=w_sc[:, i, :],
+                    rhs=vw[:, g * DV : (g + 1) * DV].bitcast(FP8X4),
+                    rhs_scale=vsc[:, g * DV : (g + 1) * DV],
+                    start=(g == 0),
+                    stop=(g == PAGES - 1),
+                )
 
-        for i in range(len(steps) + 1):
-            if i < len(steps):
-                weigh(*steps[i])
-            if i == len(steps) - 1:
-                nc.vector.tensor_reduce(total[:], sums[:], AX.X, ALU.add)
-            if i >= 1:
-                multiply(*steps[i - 1])
-            if i == len(steps) - 1:
-                nc.vector.reciprocal(inv[:], total[:])
+        for i in range(5):
+            weigh_on_vector(*steps[i])
+        multiply(0, 4)
+        nc.vector.tensor_reduce(total[:], sums[:], AX.X, ALU.add)
+        weigh_on_vector(*steps[5])
+        nc.vector.reciprocal(inv[:], total[:])
+        multiply(4, 6)
 
         out_view = out[0].rearrange("(p c) e -> p c e", c=HALVES)
         for c in range(HALVES):

@@ -30,33 +30,25 @@ def tile_attend_pkv8_soft_sink_kb_kernel(
     nc = tc.nc
     with ExitStack() as ctx:
         sb = ctx.enter_context(tc.tile_pool(name="sb", bufs=1))
+        ov = ctx.enter_context(tc.tile_pool(name="ov", bufs=1))
         ps = ctx.enter_context(tc.psum_pool(name="ps", bufs=1))
 
         offs_t = sb.tile([P, N // 16], U16, name="offs_t")
         voffs_t = sb.tile([P, PAGES * DV // 16], U16, name="voffs_t")
-        kw_pool = sb.tile([P, T], I32, name="kw_pool")
-        ks_pool = sb.tile([P, T], U8, name="ks_pool")
         vsc_pool = sb.tile([P, T // PAGE * DV], U8, name="vsc_pool")
         kb_pool = sb.tile([P, T], F32, name="kb_pool")
-        zero = sb.tile([P, 1], F32, name="zero")
-        q_raw = sb.tile([P, PACK, NQ], F32, name="q_raw")
         vs_pool = sb.tile([P, T], F32, name="vs_pool")
-        sink_t = sb.tile([P, HALVES], F32, name="sink_t")
-        ident = sb.tile([P, P], F32, name="ident")
+        zero = sb.tile([P, 1], F32, name="zero", tag="zero_then_sink")
         warm = sb.tile([P, 1], F32, name="warm")
-
+        q_raw = sb.tile([P, PACK, NQ], F32, name="q_raw")
+        ident = sb.tile([P, P], F32, name="ident")
         q_bf = sb.tile([P, HALVES, P, PACK], BF16, name="q_bf", tag="q_bf_then_vw", align_bytes=64)
         q_codes = sb.tile([P, NQ], U32, name="q_codes", align_bytes=64)
         q_sc = sb.tile([P, NQ], U8, name="q_sc", align_bytes=64)
-        kw = sb.tile([P, N], U32, name="kw", align_bytes=64)
         ks = sb.tile([P, N], U8, name="ks", align_bytes=64)
-        vw = sb.tile([P, PAGES * DV], U32, name="vw", align_bytes=64)
-        vsc = sb.tile([P, PAGES * DV], U8, name="vsc", align_bytes=64)
         kb_row = sb.tile([P, N], F32, name="kb_row")
-        vs_row = sb.tile([P, N], F32, name="vs_row")
         kb_col = [sb.tile([P, PACK], F32, name=f"kb_col{g}") for g in range(PAGES)]
         vs_col = [sb.tile([P, PACK], F32, name=f"vs_col{g}") for g in range(PAGES)]
-        s_turned = sb.tile([P, HALVES, PAGES, PACK, P], F32, name="s_turned")
         neg_s = sb.tile([P, HALVES, PAGES, PAGE], F32, name="neg_s")
         prob = sb.tile([P, HALVES, PAGES, PAGE], F32, name="prob")
         w_bf = sb.tile([P, HALVES * PAGES, P, PACK], BF16, name="w_bf", align_bytes=64)
@@ -69,48 +61,60 @@ def tile_attend_pkv8_soft_sink_kb_kernel(
         inv = sb.tile([P, HALVES], F32, name="inv")
         y_sb = sb.tile([P, HALVES, DV], F32, name="y_sb")
 
-        def page_offs(g):
-            return offs_t[:, g * PAGE // 16 : (g + 1) * PAGE // 16]
+        KW_BYTES = 4 * T
+        kw_pool = ov.tile([P, T], I32, name="kw_pool", offset=0, align_bytes=64)
+        KS_AT = 24576
+        ks_pool = ov.tile([P, T], U8, name="ks_pool", offset=KS_AT, align_bytes=64)
+        s_turned = [sb.tile([P, PACK, NQ], F32, name=f"s_turned{g}") for g in range(PAGES - 1)]
+        s_turned.append(ov.tile([P, PACK, NQ], F32, name="s_turned_last", offset=KW_BYTES, align_bytes=64))
+
+        def page_offs(lo, hi):
+            return offs_t[:, lo * PAGE // 16 : hi * PAGE // 16]
 
         def page_cols(g):
             return slice(g * PAGE, (g + 1) * PAGE)
 
-        nc.vector.memset(ks_pool[:].bitcast(I32), 0)
-        nc.vector.memset(zero[:], 0.0)
+        nc.gpsimd.memset(ks_pool[:].bitcast(I32), 0)
         nc.vector.memset(kb_pool[0:LIVE, :], 0.0)
         vs_pieces = vs_pool[0:LIVE, :].rearrange("p (a x) -> p a x", a=8)
-        nc.vector.memset(vs_pieces[:, :, 0:8], 0.0)
-        nc.scalar.activation(warm[:], zero[:], ACT.Exp)
-        make_identity(nc, ident[:])
-        for a in range(8):
+        nc.gpsimd.memset(vs_pieces[:, 0, :], 0.0)
+        nc.gpsimd.memset(zero[:], 0.0)
+        for a in range(1, 8):
             nc.gpsimd.memset(vs_pieces[:, a, :], 0.0)
+        make_identity(nc, ident[:])
+        nc.gpsimd.memset(vsc_pool[:].bitcast(I32), 0)
 
         nc.sync.dma_start(offs_t[:], offs)
         nc.sync.dma_start(kb_pool[LIVE:P, :], kb[0:1, :])
-        nc.sync.dma_start(q_raw[:], qT[0].rearrange("(p j) q -> p j q", j=PACK))
         for a in range(4):
             nc.scalar.dma_start(
                 ks_pool[32 * a : 32 * a + 4, :].bitcast(I32), k_scales[0, 4 * a : 4 * a + 4, :].bitcast(I32)
             )
-        nc.sync.dma_start(kw_pool[:], k_words[0].rearrange("p t r -> p (t r)").bitcast(I32))
-        nc.sync.dma_start(vs_pool[LIVE:P, :], vs[0:1, :])
+        nc.scalar.activation(warm[:], zero[:], ACT.Exp)
+        sink_t = sb.tile([P, HALVES], F32, name="sink_t", tag="zero_then_sink")
         nc.sync.dma_start(sink_t[:], sink[0].rearrange("(p c) o -> p (c o)", c=HALVES))
+        nc.sync.dma_start(vs_pool[LIVE:P, :], vs[0:1, :])
         nc.sync.dma_start(voffs_t[:], voffs)
+        nc.sync.dma_start(q_raw[:], qT[0].rearrange("(p j) q -> p j q", j=PACK))
+        nc.sync.dma_start(kw_pool[:], k_words[0].rearrange("p t r -> p (t r)").bitcast(I32))
+        for a in range(4):
+            nc.sync.dma_start(
+                vsc_pool[32 * a : 32 * a + 4, :].bitcast(I32).rearrange("f (u e) -> f u e", e=DV // 4),
+                v_scales[:, 4 * a : 4 * a + 4, :].rearrange("u f e -> f u e").bitcast(I32),
+            )
 
         q_view = q_raw[:].rearrange("p j (m c) -> p c m j", c=HALVES)
         for c in range(HALVES):
             nc.scalar.copy(q_bf[:, c], q_view[:, c])
 
-        def gather_kb(g):
-            nc.vector.tensor_copy(kb_row[:, page_cols(g)], kb_pool[:].indirect(page_offs(g)))
-            bank = ps.tile([P, PACK, P], F32, name="kb_bank", tag=f"bank{5 + g}")
+        for g in range(PAGES):
+            nc.vector.tensor_copy(kb_row[:, page_cols(g)], kb_pool[:].indirect(page_offs(g, g + 1)))
+            bank = ps.tile([P, PACK, P], F32, name="kb_bank", tag=f"bank{4 + g}")
             for j in range(PACK):
                 lo = g * PAGE + j * P
                 nc.tensor.transpose(bank[:, j, :], kb_row[:, lo : lo + P], ident[:])
             nc.scalar.copy(kb_col[g][:], bank[:, :, LIVE])
 
-        for g in range(PAGES):
-            gather_kb(g)
         nc.vector.tensor_copy(ks[:], ks_pool[:].indirect(offs_t[:]))
         nc.vector.quantize_mx(
             out=q_codes[:].bitcast(FP8X4), scales=q_sc[:], in_=q_bf[:].rearrange("p c m j -> p (c m j)")
@@ -120,69 +124,84 @@ def tile_attend_pkv8_soft_sink_kb_kernel(
             vw_pool[:].rearrange("p (u e) -> p u e", e=DV),
             v_words.rearrange("u p e r -> p u (e r)").bitcast(I32),
         )
-        nc.vector.tensor_copy(kw[:], kw_pool[:].bitcast(U32).indirect(offs_t[:]))
+        nc.gpsimd.tensor_scalar(neg_sink[:], sink_t[:], -1.0, 0.0, ALU.mult, ALU.add)
 
-        nc.vector.memset(vsc_pool[:].bitcast(I32), 0)
-        for a in range(4):
-            nc.sync.dma_start(
-                vsc_pool[32 * a : 32 * a + 4, :].bitcast(I32).rearrange("f (u e) -> f u e", e=DV // 4),
-                v_scales[:, 4 * a : 4 * a + 4, :].rearrange("u f e -> f u e").bitcast(I32),
-            )
+        kw = [
+            ov.tile([P, PAGE], U32, name=f"kw{g}", offset=KS_AT - 1024 + 2048 * g, align_bytes=64)
+            for g in range(PAGES)
+        ]
+        score_banks = ((0, 1), (2, 3), (2, 3))
+        turn_banks = ((4, 5), (6, 7), (0, 1))
 
-        nc.vector.tensor_scalar(neg_sink[:], sink_t[:], -1.0, None, ALU.mult)
+        def scores(g):
+            nc.vector.tensor_copy(kw[g][:], kw_pool[:].bitcast(U32).indirect(page_offs(g, g + 1)))
+            for pair in range(2):
+                bank = ps.tile([P, 2, NQ], F32, name="score", tag=f"bank{score_banks[g][pair]}")
+                for jj in range(2):
+                    j = 2 * pair + jj
+                    nc.tensor.matmul_mx(
+                        out=bank[:, jj, :],
+                        lhsT=kw[g][:, j * P : (j + 1) * P].bitcast(FP8X4),
+                        lhsT_scale=ks[:, g * PAGE + j * P : g * PAGE + (j + 1) * P],
+                        rhs=q_codes[:].bitcast(FP8X4),
+                        rhs_scale=q_sc[:],
+                        start=True,
+                        stop=True,
+                    )
+                for jj in range(2):
+                    j = 2 * pair + jj
+                    nc.scalar.activation(
+                        s_turned[g][:, j, :], bank[:, jj, :], ACT.Identity, bias=kb_col[g][:, j : j + 1]
+                    )
 
-        steps = [(c, g) for c in range(HALVES) for g in range(PAGES)]
+        turned = {}
 
-        def scores(i):
-            c, g = steps[i]
-            bank = ps.tile([P, PACK, P], F32, name="score", tag=f"bank{i}")
-            for j in range(PACK):
-                cols = slice(g * PAGE + j * P, g * PAGE + (j + 1) * P)
-                nc.tensor.matmul_mx(
-                    out=bank[:, j, :],
-                    lhsT=kw[:, cols].bitcast(FP8X4),
-                    lhsT_scale=ks[:, cols],
-                    rhs=q_codes[:, c * P : (c + 1) * P].bitcast(FP8X4),
-                    rhs_scale=q_sc[:, c * P : (c + 1) * P],
-                    start=True,
-                    stop=True,
+        def turn(g):
+            for c in range(HALVES):
+                bank = ps.tile([P, PAGE], F32, name="turn1", tag=f"bank{turn_banks[g][c]}")
+                turned[g, c] = bank
+                for j in range(PACK):
+                    nc.tensor.transpose(
+                        bank[:, j * P : (j + 1) * P], s_turned[g][:, j, c * P : (c + 1) * P], ident[:]
+                    )
+
+        def row_min(g):
+            for c in range(HALVES):
+                nc.vector.tensor_scalar(
+                    neg_s[:, c, g, :].rearrange("q (t s) -> q t s", t=PACK),
+                    turned[g, c][:].rearrange("q (s t) -> q t s", t=PACK),
+                    -1.0,
+                    neg_sink[:, c : c + 1] if g == 0 else mins[:, c, g - 1 : g],
+                    ALU.mult,
+                    ALU.min,
+                    accum_out=mins[:, c, g : g + 1],
                 )
-            for j in range(PACK):
-                nc.scalar.activation(
-                    s_turned[:, c, g, j, :], bank[:, j, :], ACT.Identity, bias=kb_col[g][:, j : j + 1]
-                )
 
-        def turn_and_min(i):
-            c, g = steps[i]
-            bank = ps.tile([P, PAGE], F32, name="turn1", tag=f"bank{i}")
-            for j in range(PACK):
-                nc.tensor.transpose(bank[:, j * P : (j + 1) * P], s_turned[:, c, g, j, :], ident[:])
-            nc.vector.tensor_scalar(
-                neg_s[:, c, g, :].rearrange("q (t s) -> q t s", t=PACK),
-                bank[:].rearrange("q (s t) -> q t s", t=PACK),
-                -1.0,
-                neg_sink[:, c : c + 1] if g == 0 else mins[:, c, g - 1 : g],
-                ALU.mult,
-                ALU.min,
-                accum_out=mins[:, c, g : g + 1],
-            )
+        scores(0)
+        scores(1)
+        turn(0)
+        scores(2)
+        turn(1)
+        turn(2)
 
-        for i in range(4):
-            scores(i)
-        for i in range(2):
-            turn_and_min(i)
-        for i in range(4, 6):
-            scores(i)
-        for i in range(2, 6):
-            turn_and_min(i)
-
+        vs_first = ov.tile([P, PAGE], F32, name="vs_first", offset=0, align_bytes=64)
+        nc.vector.tensor_copy(vs_first[:], vs_pool[:].indirect(page_offs(0, 1)))
+        nc.sync.dma_start(vs_col[0][:], vs_first[LIVE:P, :])
         for g in range(PAGES):
-            nc.vector.tensor_copy(vs_row[:, page_cols(g)], vs_pool[:].indirect(page_offs(g)))
-            nc.sync.dma_start(vs_col[g][:], vs_row[LIVE:P, page_cols(g)])
+            row_min(g)
+
+        vs_rest = ov.tile([P, 2 * PAGE], F32, name="vs_rest", offset=KW_BYTES - 3072, align_bytes=64)
+        vw = ov.tile([P, PAGES * DV], U32, name="vw", offset=KW_BYTES + 1024, align_bytes=64)
+        vsc = ov.tile([P, PAGES * DV], U8, name="vsc", offset=KW_BYTES + 2560, align_bytes=64)
+        for g in range(1, PAGES):
+            nc.vector.tensor_copy(vs_rest[:, page_cols(g - 1)], vs_pool[:].indirect(page_offs(g, g + 1)))
+            nc.sync.dma_start(vs_col[g][:], vs_rest[LIVE:P, page_cols(g - 1)])
         nc.vector.tensor_copy(vw[:], vw_pool[:].bitcast(U32).indirect(voffs_t[:]))
         nc.vector.tensor_copy(vsc[:], vsc_pool[:].indirect(voffs_t[:]))
 
-        p_banks = {}
+        steps = [(c, g) for c in range(HALVES) for g in range(PAGES)]
+        p_tags = (2, 3, 4, 5, 6, 7)
+        p_banks = []
         for c in range(HALVES):
             neg_m = mins[:, c, PAGES - 1 : PAGES]
             for g in range(PAGES):
@@ -190,22 +209,22 @@ def tile_attend_pkv8_soft_sink_kb_kernel(
                     prob[:, c, g, :], neg_s[:, c, g, :], ACT.Exp, bias=neg_m, scale=-1.0,
                     accum_out=sums[:, c, g : g + 1],
                 )
-                bank = ps.tile([P, PACK, P], F32, name="turn2", tag=f"bank{steps.index((c, g))}")
-                p_banks[c, g] = bank
+                bank = ps.tile([P, PACK, P], F32, name="turn2", tag=f"bank{p_tags[len(p_banks)]}")
+                p_banks.append(bank)
                 for t in range(PACK):
                     nc.tensor.transpose(bank[:, t, :], prob[:, c, g, t * P : (t + 1) * P], ident[:])
+        for c in range(HALVES):
             nc.scalar.activation(
-                sums[:, c, PAGES : PAGES + 1], neg_sink[:, c : c + 1], ACT.Exp, bias=neg_m, scale=-1.0
+                sums[:, c, PAGES : PAGES + 1], neg_sink[:, c : c + 1], ACT.Exp,
+                bias=mins[:, c, PAGES - 1 : PAGES], scale=-1.0,
             )
-        y_banks = [ps.tile([P, DV], F32, name=f"y{c}", tag=f"bank{6 + c}") for c in range(HALVES)]
+        y_banks = [ps.tile([P, DV], F32, name=f"y{c}", tag=f"bank{c}") for c in range(HALVES)]
 
-        w_order = steps
-
-        def weigh_on_vector(c, g):
+        def weigh(i):
             nc.vector.tensor_tensor(
-                w_bf[:, w_order.index((c, g))],
-                p_banks[c, g][:].rearrange("p t q -> p q t"),
-                vs_col[g][:].unsqueeze(1).to_broadcast([P, P, PACK]),
+                w_bf[:, i],
+                p_banks[i][:].rearrange("p t q -> p q t"),
+                vs_col[steps[i][1]][:].unsqueeze(1).to_broadcast([P, P, PACK]),
                 ALU.mult,
             )
 
@@ -216,7 +235,7 @@ def tile_attend_pkv8_soft_sink_kb_kernel(
                 in_=w_bf[:].rearrange("p i q t -> p (i q t)")[:, lo * PAGE : hi * PAGE],
             )
             for i in range(lo, hi):
-                c, g = w_order[i]
+                c, g = steps[i]
                 nc.tensor.matmul_mx(
                     out=y_banks[c][:],
                     lhsT=w_codes[:, i, :].bitcast(FP8X4),
@@ -228,12 +247,13 @@ def tile_attend_pkv8_soft_sink_kb_kernel(
                 )
 
         for i in range(5):
-            weigh_on_vector(*steps[i])
+            weigh(i)
         multiply(0, 4)
         nc.vector.tensor_reduce(total[:], sums[:], AX.X, ALU.add)
-        weigh_on_vector(*steps[5])
+        weigh(5)
+        multiply(4, 5)
         nc.vector.reciprocal(inv[:], total[:])
-        multiply(4, 6)
+        multiply(5, 6)
 
         out_view = out[0].rearrange("(p c) e -> p c e", c=HALVES)
         for c in range(HALVES):

@@ -38,7 +38,6 @@ def tile_attend_pkv8_soft_sink_kb_kernel(
         vsc_pool = sb.tile([P, T // PAGE * DV], U8, name="vsc_pool")
         kb_pool = sb.tile([P, T], F32, name="kb_pool")
         vs_pool = sb.tile([P, T], F32, name="vs_pool")
-        zero = sb.tile([P, 1], F32, name="zero", tag="zero_then_sink")
         warm = sb.tile([P, 1], F32, name="warm")
         q_raw = sb.tile([P, PACK, NQ], F32, name="q_raw")
         ident = sb.tile([P, P], F32, name="ident")
@@ -74,15 +73,9 @@ def tile_attend_pkv8_soft_sink_kb_kernel(
         def page_cols(g):
             return slice(g * PAGE, (g + 1) * PAGE)
 
-        nc.gpsimd.memset(ks_pool[:].bitcast(I32), 0)
+        nc.vector.memset(ks_pool[:].bitcast(I32), 0)
         nc.vector.memset(kb_pool[0:LIVE, :], 0.0)
-        vs_pieces = vs_pool[0:LIVE, :].rearrange("p (a x) -> p a x", a=8)
-        nc.gpsimd.memset(vs_pieces[:, 0, :], 0.0)
-        nc.gpsimd.memset(zero[:], 0.0)
-        for a in range(1, 8):
-            nc.gpsimd.memset(vs_pieces[:, a, :], 0.0)
         make_identity(nc, ident[:])
-        nc.gpsimd.memset(vsc_pool[:].bitcast(I32), 0)
 
         nc.sync.dma_start(offs_t[:], offs)
         nc.sync.dma_start(kb_pool[LIVE:P, :], kb[0:1, :])
@@ -90,18 +83,13 @@ def tile_attend_pkv8_soft_sink_kb_kernel(
             nc.scalar.dma_start(
                 ks_pool[32 * a : 32 * a + 4, :].bitcast(I32), k_scales[0, 4 * a : 4 * a + 4, :].bitcast(I32)
             )
-        nc.scalar.activation(warm[:], zero[:], ACT.Exp)
-        sink_t = sb.tile([P, HALVES], F32, name="sink_t", tag="zero_then_sink")
-        nc.sync.dma_start(sink_t[:], sink[0].rearrange("(p c) o -> p (c o)", c=HALVES))
-        nc.sync.dma_start(vs_pool[LIVE:P, :], vs[0:1, :])
+        nc.scalar.activation(warm[0:LIVE, :], kb_pool[0:LIVE, 0:1], ACT.Exp)
+        sink_t = sb.tile([P, HALVES], F32, name="sink_t")
         nc.sync.dma_start(voffs_t[:], voffs)
+        nc.sync.dma_start(sink_t[:], sink[0].rearrange("(p c) o -> p (c o)", c=HALVES))
         nc.sync.dma_start(q_raw[:], qT[0].rearrange("(p j) q -> p j q", j=PACK))
         nc.sync.dma_start(kw_pool[:], k_words[0].rearrange("p t r -> p (t r)").bitcast(I32))
-        for a in range(4):
-            nc.sync.dma_start(
-                vsc_pool[32 * a : 32 * a + 4, :].bitcast(I32).rearrange("f (u e) -> f u e", e=DV // 4),
-                v_scales[:, 4 * a : 4 * a + 4, :].rearrange("u f e -> f u e").bitcast(I32),
-            )
+        nc.sync.dma_start(vs_pool[:], vs)
 
         q_view = q_raw[:].rearrange("p j (m c) -> p c m j", c=HALVES)
         for c in range(HALVES):
@@ -124,6 +112,12 @@ def tile_attend_pkv8_soft_sink_kb_kernel(
             vw_pool[:].rearrange("p (u e) -> p u e", e=DV),
             v_words.rearrange("u p e r -> p u (e r)").bitcast(I32),
         )
+        nc.vector.memset(vsc_pool[:].bitcast(I32), 0)
+        for a in range(4):
+            nc.sync.dma_start(
+                vsc_pool[32 * a : 32 * a + 4, :].bitcast(I32).rearrange("f (u e) -> f u e", e=DV // 4),
+                v_scales[:, 4 * a : 4 * a + 4, :].rearrange("u f e -> f u e").bitcast(I32),
+            )
         nc.gpsimd.tensor_scalar(neg_sink[:], sink_t[:], -1.0, 0.0, ALU.mult, ALU.add)
 
         kw = [

@@ -35,27 +35,22 @@ def tile_attend_pkv8_soft_sink_kb_kernel(
 
         offs_t = sb.tile([P, N // 16], U16, name="offs_t")
         voffs_t = sb.tile([P, PAGES * DV // 16], U16, name="voffs_t")
-        vsc_pool = sb.tile([P, T // PAGE * DV], U8, name="vsc_pool")
         kb_pool = sb.tile([P, T], F32, name="kb_pool")
-        vs_pool = sb.tile([P, T], F32, name="vs_pool")
         warm = sb.tile([P, 1], F32, name="warm")
         q_raw = sb.tile([P, PACK, NQ], F32, name="q_raw")
         ident = sb.tile([P, P], F32, name="ident")
-        q_bf = sb.tile([P, HALVES, P, PACK], BF16, name="q_bf", tag="q_bf_then_vw", align_bytes=64)
+        q_bf = sb.tile([P, HALVES, P, PACK], BF16, name="q_bf", align_bytes=64)
         q_codes = sb.tile([P, NQ], U32, name="q_codes", align_bytes=64)
         q_sc = sb.tile([P, NQ], U8, name="q_sc", align_bytes=64)
         ks = sb.tile([P, N], U8, name="ks", align_bytes=64)
         kb_row = sb.tile([P, N], F32, name="kb_row")
         kb_col = [sb.tile([P, PACK], F32, name=f"kb_col{g}") for g in range(PAGES)]
         vs_col = [sb.tile([P, PACK], F32, name=f"vs_col{g}") for g in range(PAGES)]
-        neg_s = sb.tile([P, HALVES, PAGES, PAGE], F32, name="neg_s")
-        prob = sb.tile([P, HALVES, PAGES, PAGE], F32, name="prob")
         w_bf = sb.tile([P, HALVES * PAGES, P, PACK], BF16, name="w_bf", align_bytes=64)
         w_codes = sb.tile([P, HALVES * PAGES, P], U32, name="w_codes", align_bytes=64)
         w_sc = sb.tile([P, HALVES * PAGES, P], U8, name="w_sc", align_bytes=64)
-        mins = sb.tile([P, HALVES, PAGES], F32, name="mins")
-        neg_sink = sb.tile([P, HALVES], F32, name="neg_sink")
-        sums = sb.tile([P, HALVES, PAGES + 1], F32, name="sums")
+        neg_s_last = sb.tile([P, HALVES, PAGE + 8], F32, name="neg_s_last")
+        sums = sb.tile([P, HALVES, PAGES], F32, name="sums")
         total = sb.tile([P, HALVES], F32, name="total")
         inv = sb.tile([P, HALVES], F32, name="inv")
         y_sb = sb.tile([P, HALVES, DV], F32, name="y_sb")
@@ -64,8 +59,9 @@ def tile_attend_pkv8_soft_sink_kb_kernel(
         kw_pool = ov.tile([P, T], I32, name="kw_pool", offset=0, align_bytes=64)
         KS_AT = 24576
         ks_pool = ov.tile([P, T], U8, name="ks_pool", offset=KS_AT, align_bytes=64)
-        s_turned = [sb.tile([P, PACK, NQ], F32, name=f"s_turned{g}") for g in range(PAGES - 1)]
-        s_turned.append(ov.tile([P, PACK, NQ], F32, name="s_turned_last", offset=KW_BYTES, align_bytes=64))
+        vw_pool = sb.tile([P, T // PAGE * DV], I32, name="vw_pool")
+        vsc_pool = sb.tile([P, T // PAGE * DV], U8, name="vsc_pool")
+        s_turned = [sb.tile([P, PACK, NQ], F32, name=f"s_turned{g}") for g in range(PAGES)]
 
         def page_offs(lo, hi):
             return offs_t[:, lo * PAGE // 16 : hi * PAGE // 16]
@@ -86,10 +82,15 @@ def tile_attend_pkv8_soft_sink_kb_kernel(
         nc.scalar.activation(warm[0:LIVE, :], kb_pool[0:LIVE, 0:1], ACT.Exp)
         sink_t = sb.tile([P, HALVES], F32, name="sink_t")
         nc.sync.dma_start(voffs_t[:], voffs)
-        nc.sync.dma_start(sink_t[:], sink[0].rearrange("(p c) o -> p (c o)", c=HALVES))
         nc.sync.dma_start(q_raw[:], qT[0].rearrange("(p j) q -> p j q", j=PACK))
         nc.sync.dma_start(kw_pool[:], k_words[0].rearrange("p t r -> p (t r)").bitcast(I32))
+        vs_pool = sb.tile([P, T], F32, name="vs_pool")
         nc.sync.dma_start(vs_pool[:], vs)
+        nc.sync.dma_start(
+            vw_pool[:].rearrange("p (u e) -> p u e", e=DV),
+            v_words.rearrange("u p e r -> p u (e r)").bitcast(I32),
+        )
+        nc.sync.dma_start(sink_t[:], sink[0].rearrange("(p c) o -> p (c o)", c=HALVES))
 
         q_view = q_raw[:].rearrange("p j (m c) -> p c m j", c=HALVES)
         for c in range(HALVES):
@@ -107,18 +108,13 @@ def tile_attend_pkv8_soft_sink_kb_kernel(
         nc.vector.quantize_mx(
             out=q_codes[:].bitcast(FP8X4), scales=q_sc[:], in_=q_bf[:].rearrange("p c m j -> p (c m j)")
         )
-        vw_pool = sb.tile([P, T // PAGE * DV], I32, name="vw_pool", tag="q_bf_then_vw", align_bytes=64)
-        nc.sync.dma_start(
-            vw_pool[:].rearrange("p (u e) -> p u e", e=DV),
-            v_words.rearrange("u p e r -> p u (e r)").bitcast(I32),
-        )
         nc.vector.memset(vsc_pool[:].bitcast(I32), 0)
         for a in range(4):
             nc.sync.dma_start(
                 vsc_pool[32 * a : 32 * a + 4, :].bitcast(I32).rearrange("f (u e) -> f u e", e=DV // 4),
                 v_scales[:, 4 * a : 4 * a + 4, :].rearrange("u f e -> f u e").bitcast(I32),
             )
-        nc.gpsimd.tensor_scalar(neg_sink[:], sink_t[:], -1.0, 0.0, ALU.mult, ALU.add)
+        nc.gpsimd.tensor_scalar(neg_s_last[:, :, PAGE], sink_t[:], -1.0, 0.0, ALU.mult, ALU.add)
 
         kw = [
             ov.tile([P, PAGE], U32, name=f"kw{g}", offset=KS_AT - 1024 + 2048 * g, align_bytes=64)
@@ -159,17 +155,28 @@ def tile_attend_pkv8_soft_sink_kb_kernel(
                         bank[:, j * P : (j + 1) * P], s_turned[g][:, j, c * P : (c + 1) * P], ident[:]
                     )
 
-        def row_min(g):
-            for c in range(HALVES):
-                nc.vector.tensor_scalar(
-                    neg_s[:, c, g, :].rearrange("q (t s) -> q t s", t=PACK),
-                    turned[g, c][:].rearrange("q (s t) -> q t s", t=PACK),
-                    -1.0,
-                    neg_sink[:, c : c + 1] if g == 0 else mins[:, c, g - 1 : g],
-                    ALU.mult,
-                    ALU.min,
-                    accum_out=mins[:, c, g : g + 1],
-                )
+        neg_s = {}
+        mins = {}
+        MIN_AT = (36864, 45056)
+
+        def row_min(g, c):
+            if g == PAGES - 1:
+                neg_s[g, c] = neg_s_last[:, c, :]
+            else:
+                neg_s[g, c] = sb.tile([P, PAGE], F32, name=f"neg_s{g}{c}")[:]
+            if g == 1:
+                mins[g, c] = ov.tile([P, 128], F32, name=f"min_mid{c}", offset=MIN_AT[c], align_bytes=64)
+            else:
+                mins[g, c] = sb.tile([P, 1], F32, name=f"min{g}{c}")
+            nc.vector.tensor_scalar(
+                neg_s[g, c][:, 0:PAGE].rearrange("q (t s) -> q t s", t=PACK),
+                turned[g, c][:].rearrange("q (s t) -> q t s", t=PACK),
+                -1.0,
+                neg_s_last[:, c, PAGE : PAGE + 1] if g == 0 else mins[g - 1, c][:, 0:1],
+                ALU.mult,
+                ALU.min,
+                accum_out=mins[g, c][:, 0:1],
+            )
 
         scores(0)
         scores(1)
@@ -178,47 +185,64 @@ def tile_attend_pkv8_soft_sink_kb_kernel(
         turn(1)
         turn(2)
 
-        vs_first = ov.tile([P, PAGE], F32, name="vs_first", offset=0, align_bytes=64)
-        nc.vector.tensor_copy(vs_first[:], vs_pool[:].indirect(page_offs(0, 1)))
-        nc.sync.dma_start(vs_col[0][:], vs_first[LIVE:P, :])
-        for g in range(PAGES):
-            row_min(g)
+        vs_at = (0, MIN_AT[0], MIN_AT[1] + 64 - 4 * PAGE)
 
-        vs_rest = ov.tile([P, 2 * PAGE], F32, name="vs_rest", offset=KW_BYTES - 3072, align_bytes=64)
-        vw = ov.tile([P, PAGES * DV], U32, name="vw", offset=KW_BYTES + 1024, align_bytes=64)
-        vsc = ov.tile([P, PAGES * DV], U8, name="vsc", offset=KW_BYTES + 2560, align_bytes=64)
-        for g in range(1, PAGES):
-            nc.vector.tensor_copy(vs_rest[:, page_cols(g - 1)], vs_pool[:].indirect(page_offs(g, g + 1)))
-            nc.sync.dma_start(vs_col[g][:], vs_rest[LIVE:P, page_cols(g - 1)])
+        def gather_vs(g):
+            row = ov.tile([P, PAGE], F32, name=f"vs_row{g}", offset=vs_at[g], align_bytes=64)
+            nc.vector.tensor_copy(row[:], vs_pool[:].indirect(page_offs(g, g + 1)))
+            nc.sync.dma_start(vs_col[g][:], row[LIVE:P, :])
+
+        gather_vs(0)
+        for g in range(PAGES - 1):
+            for c in range(HALVES):
+                row_min(g, c)
+        row_min(2, 0)
+        gather_vs(1)
+        row_min(2, 1)
+        gather_vs(2)
+        vw = ov.tile([P, PAGES * DV], U32, name="vw", offset=MIN_AT[1] + 448, align_bytes=64)
+        vsc = ov.tile([P, PAGES * DV], U8, name="vsc", offset=MIN_AT[1] + 64, align_bytes=64)
         nc.vector.tensor_copy(vw[:], vw_pool[:].bitcast(U32).indirect(voffs_t[:]))
         nc.vector.tensor_copy(vsc[:], vsc_pool[:].indirect(voffs_t[:]))
 
-        steps = [(c, g) for c in range(HALVES) for g in range(PAGES)]
-        p_tags = (2, 3, 4, 5, 6, 7)
-        p_banks = []
+        first_banks = [ps.tile([P, 2, NQ], F32, name="turn2_first", tag=f"bank{2 + u}") for u in range(2)]
+        p_tags = {(1, 0): 4, (2, 0): 5, (1, 1): 6, (2, 1): 7}
+        p_banks = {}
         for c in range(HALVES):
-            neg_m = mins[:, c, PAGES - 1 : PAGES]
             for g in range(PAGES):
+                width = PAGE + 1 if g == PAGES - 1 else PAGE
+                prob = sb.tile([P, width], F32, name=f"prob{g}{c}")
                 nc.scalar.activation(
-                    prob[:, c, g, :], neg_s[:, c, g, :], ACT.Exp, bias=neg_m, scale=-1.0,
+                    prob[:], neg_s[g, c][:, 0:width], ACT.Exp, bias=mins[PAGES - 1, c][:], scale=-1.0,
                     accum_out=sums[:, c, g : g + 1],
                 )
-                bank = ps.tile([P, PACK, P], F32, name="turn2", tag=f"bank{p_tags[len(p_banks)]}")
-                p_banks.append(bank)
+                if g > 0:
+                    p_banks[g, c] = ps.tile([P, PACK, P], F32, name="turn2", tag=f"bank{p_tags[g, c]}")
                 for t in range(PACK):
-                    nc.tensor.transpose(bank[:, t, :], prob[:, c, g, t * P : (t + 1) * P], ident[:])
-        for c in range(HALVES):
-            nc.scalar.activation(
-                sums[:, c, PAGES : PAGES + 1], neg_sink[:, c : c + 1], ACT.Exp,
-                bias=mins[:, c, PAGES - 1 : PAGES], scale=-1.0,
-            )
+                    if g == 0:
+                        dst = first_banks[t // 2][:, t % 2, c * P : (c + 1) * P]
+                    else:
+                        dst = p_banks[g, c][:, t, :]
+                    nc.tensor.transpose(dst, prob[:, t * P : (t + 1) * P], ident[:])
         y_banks = [ps.tile([P, DV], F32, name=f"y{c}", tag=f"bank{c}") for c in range(HALVES)]
+
+        steps = [(1, 0), (1, 1), (2, 0), (0, 0), (0, 1), (2, 1)]
+
+        w_planes = sb.tile([P, PACK, NQ], BF16, name="w_planes")
+        for t in range(PACK):
+            nc.scalar.activation(
+                w_planes[:, t, :], first_banks[t // 2][:, t % 2, :], ACT.Copy, scale=vs_col[0][:, t : t + 1]
+            )
+        nc.scalar.copy(
+            w_bf[:, 3:5].rearrange("p c (a i) t -> p (c a) t i", i=4),
+            w_planes[:].rearrange("p t (a i) -> p a t i", i=4),
+        )
 
         def weigh(i):
             nc.vector.tensor_tensor(
                 w_bf[:, i],
-                p_banks[i][:].rearrange("p t q -> p q t"),
-                vs_col[steps[i][1]][:].unsqueeze(1).to_broadcast([P, P, PACK]),
+                p_banks[steps[i]][:].rearrange("p t q -> p q t"),
+                vs_col[steps[i][0]][:].unsqueeze(1).to_broadcast([P, P, PACK]),
                 ALU.mult,
             )
 
@@ -229,25 +253,26 @@ def tile_attend_pkv8_soft_sink_kb_kernel(
                 in_=w_bf[:].rearrange("p i q t -> p (i q t)")[:, lo * PAGE : hi * PAGE],
             )
             for i in range(lo, hi):
-                c, g = steps[i]
+                g, c = steps[i]
                 nc.tensor.matmul_mx(
                     out=y_banks[c][:],
                     lhsT=w_codes[:, i, :].bitcast(FP8X4),
                     lhsT_scale=w_sc[:, i, :],
                     rhs=vw[:, g * DV : (g + 1) * DV].bitcast(FP8X4),
                     rhs_scale=vsc[:, g * DV : (g + 1) * DV],
-                    start=(g == 0),
-                    stop=(g == PAGES - 1),
+                    start=(i < HALVES),
+                    stop=(i in (3, 5)),
                 )
 
-        for i in range(5):
-            weigh(i)
-        multiply(0, 4)
+        weigh(0)
+        weigh(1)
+        weigh(2)
+        multiply(0, 2)
         nc.vector.tensor_reduce(total[:], sums[:], AX.X, ALU.add)
         weigh(5)
-        multiply(4, 5)
         nc.vector.reciprocal(inv[:], total[:])
-        multiply(5, 6)
+        multiply(2, 4)
+        multiply(4, 6)
 
         out_view = out[0].rearrange("(p c) e -> p c e", c=HALVES)
         for c in range(HALVES):

@@ -81,20 +81,29 @@ def tile_attend_pkv8_soft_sink_kb_kernel(
             )
         nc.scalar.activation(warm[0:LIVE, :], kb_pool[0:LIVE, 0:1], ACT.Exp)
         sink_t = sb.tile([P, HALVES], F32, name="sink_t")
+        vs_in = sb.tile([P, T // P], F32, name="vs_in")
+        nc.sync.dma_start(vs_in[:], vs[0].rearrange("(p c) -> p c", p=P))
         nc.sync.dma_start(voffs_t[:], voffs)
+        nc.sync.dma_start(sink_t[:], sink[0].rearrange("(p c) o -> p (c o)", c=HALVES))
         nc.sync.dma_start(q_raw[:], qT[0].rearrange("(p j) q -> p j q", j=PACK))
         nc.sync.dma_start(kw_pool[:], k_words[0].rearrange("p t r -> p (t r)").bitcast(I32))
         vs_pool = sb.tile([P, T], F32, name="vs_pool")
-        nc.sync.dma_start(vs_pool[:], vs)
         nc.sync.dma_start(
             vw_pool[:].rearrange("p (u e) -> p u e", e=DV),
             v_words.rearrange("u p e r -> p u (e r)").bitcast(I32),
         )
-        nc.sync.dma_start(sink_t[:], sink[0].rearrange("(p c) o -> p (c o)", c=HALVES))
 
         q_view = q_raw[:].rearrange("p j (m c) -> p c m j", c=HALVES)
         for c in range(HALVES):
             nc.scalar.copy(q_bf[:, c], q_view[:, c])
+
+        vs_runs = vs_pool[:].rearrange("p (n a t) -> p a n t", n=P, t=PACK)
+        for a in range(T // PAGE):
+            bank = ps.tile([P, PACK, P], F32, name="vs_bank", tag=f"bank{a % 4}")
+            for t in range(PACK):
+                col = PACK * a + t
+                nc.tensor.transpose(bank[:, t, :], vs_in[:, col : col + 1].to_broadcast([P, P]), ident[:])
+            nc.scalar.activation(vs_runs[:, a], bank[:].rearrange("p t n -> p n t"), ACT.Copy)
 
         for g in range(PAGES):
             nc.vector.tensor_copy(kb_row[:, page_cols(g)], kb_pool[:].indirect(page_offs(g, g + 1)))
@@ -234,8 +243,8 @@ def tile_attend_pkv8_soft_sink_kb_kernel(
                 w_planes[:, t, :], first_banks[t // 2][:, t % 2, :], ACT.Copy, scale=vs_col[0][:, t : t + 1]
             )
         nc.scalar.copy(
-            w_bf[:, 3:5].rearrange("p c (a i) t -> p (c a) t i", i=4),
-            w_planes[:].rearrange("p t (a i) -> p a t i", i=4),
+            w_bf[:, 3:5].rearrange("p c q t -> p (c q) t"),
+            w_planes[:].rearrange("p t q -> p q t"),
         )
 
         def weigh(i):

@@ -20,8 +20,19 @@ NQ, N, T, D, DV = 256, 1536, 4096, 512, 128
 PAGE = 512
 PAGES = N // PAGE
 HALVES = NQ // P
+LAST = PAGES - 1
 LIVE = P - 1
+QUADRANTS = 4
+LIST_COLS = PAGE // 16
+WORD = 4
+
+KW_AT = 0
+Q_RAW_AT = KW_AT + PAGE * WORD // 2
+MIN_AT = 8192
+MIN_COLS = 32
+
 FLOPS = 2 * NQ * N * (D + DV)
+BYTES = D * NQ * 4 + T * (D + DV) + T * (D + DV) // 32 + 2 * T * 4 + NQ * 4 + P * (N + PAGES * DV) // 8 + NQ * DV * 4
 
 
 def tile_attend_pkv8_soft_sink_kb_kernel(
@@ -30,44 +41,27 @@ def tile_attend_pkv8_soft_sink_kb_kernel(
     nc = tc.nc
     with ExitStack() as ctx:
         sb = ctx.enter_context(tc.tile_pool(name="sb", bufs=1))
-        ov = ctx.enter_context(tc.tile_pool(name="ov", bufs=1))
+        reuse = ctx.enter_context(tc.tile_pool(name="reuse", bufs=1))
         ps = ctx.enter_context(tc.psum_pool(name="ps", bufs=1))
+
+        def bank_tile(shape, name, bank):
+            return ps.tile(shape, F32, name=name, tag=f"bank{bank}")
+
+        def page_offs(g):
+            return offs_t[:, g * LIST_COLS : (g + 1) * LIST_COLS]
 
         offs_t = sb.tile([P, N // 16], U16, name="offs_t")
         voffs_t = sb.tile([P, PAGES * DV // 16], U16, name="voffs_t")
-        kb_pool = sb.tile([P, T], F32, name="kb_pool")
-        warm = sb.tile([P, 1], F32, name="warm")
-        q_raw = sb.tile([P, PACK, NQ], F32, name="q_raw")
-        ident = sb.tile([P, P], F32, name="ident")
-        q_bf = sb.tile([P, HALVES, P, PACK], BF16, name="q_bf", align_bytes=64)
-        q_codes = sb.tile([P, NQ], U32, name="q_codes", align_bytes=64)
-        q_sc = sb.tile([P, NQ], U8, name="q_sc", align_bytes=64)
-        ks = sb.tile([P, N], U8, name="ks", align_bytes=64)
-        kb_row = sb.tile([P, N], F32, name="kb_row")
-        kb_col = [sb.tile([P, PACK], F32, name=f"kb_col{g}") for g in range(PAGES)]
-        vs_col = [sb.tile([P, PACK], F32, name=f"vs_col{g}") for g in range(PAGES)]
-        w_bf = sb.tile([P, HALVES * PAGES, P, PACK], BF16, name="w_bf", align_bytes=64)
-        w_codes = sb.tile([P, HALVES * PAGES, P], U32, name="w_codes", align_bytes=64)
-        w_sc = sb.tile([P, HALVES * PAGES, P], U8, name="w_sc", align_bytes=64)
-        neg_s_last = sb.tile([P, HALVES, PAGE + 8], F32, name="neg_s_last")
-        sums = sb.tile([P, HALVES, PAGES], F32, name="sums")
-        total = sb.tile([P, HALVES], F32, name="total")
-        inv = sb.tile([P, HALVES], F32, name="inv")
-        y_sb = sb.tile([P, HALVES, DV], F32, name="y_sb")
-
-        KW_BYTES = 4 * T
-        kw_pool = ov.tile([P, T], I32, name="kw_pool", offset=0, align_bytes=64)
-        KS_AT = 24576
-        ks_pool = ov.tile([P, T], U8, name="ks_pool", offset=KS_AT, align_bytes=64)
+        kw_pool = sb.tile([P, T], I32, name="kw_pool")
+        ks_pool = sb.tile([P, T], U8, name="ks_pool")
         vw_pool = sb.tile([P, T // PAGE * DV], I32, name="vw_pool")
         vsc_pool = sb.tile([P, T // PAGE * DV], U8, name="vsc_pool")
-        s_turned = [sb.tile([P, PACK, NQ], F32, name=f"s_turned{g}") for g in range(PAGES)]
-
-        def page_offs(lo, hi):
-            return offs_t[:, lo * PAGE // 16 : hi * PAGE // 16]
-
-        def page_cols(g):
-            return slice(g * PAGE, (g + 1) * PAGE)
+        kb_pool = sb.tile([P, T], F32, name="kb_pool")
+        vs_pool = sb.tile([P, T], F32, name="vs_pool")
+        vs_in = sb.tile([P, T // P], F32, name="vs_in")
+        sink_t = sb.tile([P, HALVES], F32, name="sink_t")
+        ident = sb.tile([P, P], F32, name="ident")
+        q_raw = reuse.tile([P, PACK, NQ], F32, name="q_raw", offset=Q_RAW_AT, align_bytes=64)
 
         nc.vector.memset(ks_pool[:].bitcast(I32), 0)
         nc.vector.memset(kb_pool[0:LIVE, :], 0.0)
@@ -75,67 +69,84 @@ def tile_attend_pkv8_soft_sink_kb_kernel(
 
         nc.sync.dma_start(offs_t[:], offs)
         nc.sync.dma_start(kb_pool[LIVE:P, :], kb[0:1, :])
-        for a in range(4):
+        for a in range(QUADRANTS):
             nc.scalar.dma_start(
                 ks_pool[32 * a : 32 * a + 4, :].bitcast(I32), k_scales[0, 4 * a : 4 * a + 4, :].bitcast(I32)
             )
-        nc.scalar.activation(warm[0:LIVE, :], kb_pool[0:LIVE, 0:1], ACT.Exp)
-        sink_t = sb.tile([P, HALVES], F32, name="sink_t")
-        vs_in = sb.tile([P, T // P], F32, name="vs_in")
         nc.sync.dma_start(vs_in[:], vs[0].rearrange("(p c) -> p c", p=P))
         nc.sync.dma_start(voffs_t[:], voffs)
         nc.sync.dma_start(sink_t[:], sink[0].rearrange("(p c) o -> p (c o)", c=HALVES))
         nc.sync.dma_start(q_raw[:], qT[0].rearrange("(p j) q -> p j q", j=PACK))
         nc.sync.dma_start(kw_pool[:], k_words[0].rearrange("p t r -> p (t r)").bitcast(I32))
-        vs_pool = sb.tile([P, T], F32, name="vs_pool")
         nc.sync.dma_start(
             vw_pool[:].rearrange("p (u e) -> p u e", e=DV),
             v_words.rearrange("u p e r -> p u (e r)").bitcast(I32),
         )
 
-        q_view = q_raw[:].rearrange("p j (m c) -> p c m j", c=HALVES)
-        for c in range(HALVES):
-            nc.scalar.copy(q_bf[:, c], q_view[:, c])
-
         vs_runs = vs_pool[:].rearrange("p (n a t) -> p a n t", n=P, t=PACK)
-        for a in range(T // PAGE):
-            bank = ps.tile([P, PACK, P], F32, name="vs_bank", tag=f"bank{a % 4}")
+        for a in range(T // P // PACK):
+            bank = bank_tile([P, PACK, P], "vs_bank", a % 4)
             for t in range(PACK):
                 col = PACK * a + t
                 nc.tensor.transpose(bank[:, t, :], vs_in[:, col : col + 1].to_broadcast([P, P]), ident[:])
             nc.scalar.activation(vs_runs[:, a], bank[:].rearrange("p t n -> p n t"), ACT.Copy)
 
+        q_bf = sb.tile([P, HALVES, P, PACK], BF16, name="q_bf", align_bytes=64)
+        q_view = q_raw[:].rearrange("p j (m c) -> p c m j", c=HALVES)
+        for c in range(HALVES):
+            nc.scalar.copy(q_bf[:, c], q_view[:, c])
+
+        kb_row = sb.tile([P, N], F32, name="kb_row")
+        kb_col = []
         for g in range(PAGES):
-            nc.vector.tensor_copy(kb_row[:, page_cols(g)], kb_pool[:].indirect(page_offs(g, g + 1)))
-            bank = ps.tile([P, PACK, P], F32, name="kb_bank", tag=f"bank{4 + g}")
+            nc.vector.tensor_copy(kb_row[:, g * PAGE : (g + 1) * PAGE], kb_pool[:].indirect(page_offs(g)))
+            bank = bank_tile([P, PACK, P], "kb_bank", 4 + g)
             for j in range(PACK):
-                lo = g * PAGE + j * P
-                nc.tensor.transpose(bank[:, j, :], kb_row[:, lo : lo + P], ident[:])
+                first = g * PAGE + j * P
+                nc.tensor.transpose(bank[:, j, :], kb_row[:, first : first + P], ident[:])
+            kb_col.append(sb.tile([P, PACK], F32, name=f"kb_col{g}"))
             nc.scalar.copy(kb_col[g][:], bank[:, :, LIVE])
 
+        ks = sb.tile([P, N], U8, name="ks", align_bytes=64)
         nc.vector.tensor_copy(ks[:], ks_pool[:].indirect(offs_t[:]))
+
+        vs_col = [sb.tile([P, PACK], F32, name=f"vs_col{g}") for g in range(PAGES)]
+
+        def gather_vs(g, row):
+            nc.vector.tensor_copy(row[:], vs_pool[:].indirect(page_offs(g)))
+            nc.sync.dma_start(vs_col[g][:], row[LIVE:P, :])
+
+        for g in range(LAST):
+            gather_vs(g, sb.tile([P, PAGE], F32, name=f"vs_row{g}"))
+
+        q_codes = sb.tile([P, NQ], U32, name="q_codes", align_bytes=64)
+        q_sc = sb.tile([P, NQ], U8, name="q_sc", align_bytes=64)
         nc.vector.quantize_mx(
             out=q_codes[:].bitcast(FP8X4), scales=q_sc[:], in_=q_bf[:].rearrange("p c m j -> p (c m j)")
         )
         nc.vector.memset(vsc_pool[:].bitcast(I32), 0)
-        for a in range(4):
+        for a in range(QUADRANTS):
             nc.sync.dma_start(
-                vsc_pool[32 * a : 32 * a + 4, :].bitcast(I32).rearrange("f (u e) -> f u e", e=DV // 4),
+                vsc_pool[32 * a : 32 * a + 4, :].bitcast(I32).rearrange("f (u e) -> f u e", e=DV // WORD),
                 v_scales[:, 4 * a : 4 * a + 4, :].rearrange("u f e -> f u e").bitcast(I32),
             )
+
+        neg_s_last = sb.tile([P, HALVES, PAGE + 8], F32, name="neg_s_last")
         nc.gpsimd.tensor_scalar(neg_s_last[:, :, PAGE], sink_t[:], -1.0, 0.0, ALU.mult, ALU.add)
 
         kw = [
-            ov.tile([P, PAGE], U32, name=f"kw{g}", offset=KS_AT - 1024 + 2048 * g, align_bytes=64)
+            reuse.tile([P, PAGE], U32, name=f"kw{g}", offset=KW_AT + g * PAGE * WORD, align_bytes=64)
             for g in range(PAGES)
         ]
+        s_turned = [sb.tile([P, PACK, NQ], F32, name=f"s_turned{g}") for g in range(PAGES)]
         score_banks = ((0, 1), (2, 3), (2, 3))
         turn_banks = ((4, 5), (6, 7), (0, 1))
+        turned = {}
 
         def scores(g):
-            nc.vector.tensor_copy(kw[g][:], kw_pool[:].bitcast(U32).indirect(page_offs(g, g + 1)))
-            for pair in range(2):
-                bank = ps.tile([P, 2, NQ], F32, name="score", tag=f"bank{score_banks[g][pair]}")
+            nc.vector.tensor_copy(kw[g][:], kw_pool[:].bitcast(U32).indirect(page_offs(g)))
+            for pair in range(PACK // 2):
+                bank = bank_tile([P, 2, NQ], "score", score_banks[g][pair])
                 for jj in range(2):
                     j = 2 * pair + jj
                     nc.tensor.matmul_mx(
@@ -153,136 +164,121 @@ def tile_attend_pkv8_soft_sink_kb_kernel(
                         s_turned[g][:, j, :], bank[:, jj, :], ACT.Identity, bias=kb_col[g][:, j : j + 1]
                     )
 
-        turned = {}
-
         def turn(g):
             for c in range(HALVES):
-                bank = ps.tile([P, PAGE], F32, name="turn1", tag=f"bank{turn_banks[g][c]}")
-                turned[g, c] = bank
+                turned[g, c] = bank_tile([P, PAGE], "turned", turn_banks[g][c])
                 for j in range(PACK):
                     nc.tensor.transpose(
-                        bank[:, j * P : (j + 1) * P], s_turned[g][:, j, c * P : (c + 1) * P], ident[:]
+                        turned[g, c][:, j * P : (j + 1) * P], s_turned[g][:, j, c * P : (c + 1) * P], ident[:]
                     )
+
+        scores(0)
+        for g in range(1, PAGES):
+            scores(g)
+            turn(g - 1)
+        turn(LAST)
+
+        vs_row_last = reuse.tile([P, PAGE], F32, name="vs_row_last", offset=KW_AT + PAGE * WORD, align_bytes=64)
+        gather_vs(LAST, vs_row_last)
 
         neg_s = {}
         mins = {}
-        MIN_AT = (36864, 45056)
-
-        def row_min(g, c):
-            if g == PAGES - 1:
-                neg_s[g, c] = neg_s_last[:, c, :]
-            else:
-                neg_s[g, c] = sb.tile([P, PAGE], F32, name=f"neg_s{g}{c}")[:]
-            if g == 1:
-                mins[g, c] = ov.tile([P, 128], F32, name=f"min_mid{c}", offset=MIN_AT[c], align_bytes=64)
-            else:
-                mins[g, c] = sb.tile([P, 1], F32, name=f"min{g}{c}")
-            nc.vector.tensor_scalar(
-                neg_s[g, c][:, 0:PAGE].rearrange("q (t s) -> q t s", t=PACK),
-                turned[g, c][:].rearrange("q (s t) -> q t s", t=PACK),
-                -1.0,
-                neg_s_last[:, c, PAGE : PAGE + 1] if g == 0 else mins[g - 1, c][:, 0:1],
-                ALU.mult,
-                ALU.min,
-                accum_out=mins[g, c][:, 0:1],
-            )
-
-        scores(0)
-        scores(1)
-        turn(0)
-        scores(2)
-        turn(1)
-        turn(2)
-
-        vs_at = (0, MIN_AT[0], MIN_AT[1] + 64 - 4 * PAGE)
-
-        def gather_vs(g):
-            row = ov.tile([P, PAGE], F32, name=f"vs_row{g}", offset=vs_at[g], align_bytes=64)
-            nc.vector.tensor_copy(row[:], vs_pool[:].indirect(page_offs(g, g + 1)))
-            nc.sync.dma_start(vs_col[g][:], row[LIVE:P, :])
-
-        gather_vs(0)
-        for g in range(PAGES - 1):
+        for g in range(PAGES):
             for c in range(HALVES):
-                row_min(g, c)
-        row_min(2, 0)
-        gather_vs(1)
-        row_min(2, 1)
-        gather_vs(2)
-        vw = ov.tile([P, PAGES * DV], U32, name="vw", offset=MIN_AT[1] + 448, align_bytes=64)
-        vsc = ov.tile([P, PAGES * DV], U8, name="vsc", offset=MIN_AT[1] + 64, align_bytes=64)
+                if g == LAST:
+                    neg_s[g, c] = neg_s_last[:, c, 0 : PAGE + 1]
+                else:
+                    neg_s[g, c] = sb.tile([P, PAGE], F32, name=f"neg_s{g}{c}")[:]
+                if (g, c) == (LAST - 1, 0):
+                    mins[g, c] = reuse.tile([P, MIN_COLS], F32, name="min_mid", offset=MIN_AT, align_bytes=64)
+                else:
+                    mins[g, c] = sb.tile([P, 1], F32, name=f"min{g}{c}")
+                nc.vector.tensor_scalar(
+                    neg_s[g, c][:, 0:PAGE].rearrange("q (t z) -> q t z", t=PACK),
+                    turned[g, c][:].rearrange("q (z t) -> q t z", t=PACK),
+                    -1.0,
+                    neg_s_last[:, c, PAGE : PAGE + 1] if g == 0 else mins[g - 1, c][:, 0:1],
+                    ALU.mult,
+                    ALU.min,
+                    accum_out=mins[g, c][:, 0:1],
+                )
+
+        min_half = MIN_AT + MIN_COLS * WORD // 2
+        vw = reuse.tile([P, PAGES * DV], U32, name="vw", offset=min_half, align_bytes=64)
+        vsc = reuse.tile([P, PAGES * DV], U8, name="vsc", offset=min_half - PAGES * DV, align_bytes=64)
         nc.vector.tensor_copy(vw[:], vw_pool[:].bitcast(U32).indirect(voffs_t[:]))
         nc.vector.tensor_copy(vsc[:], vsc_pool[:].indirect(voffs_t[:]))
 
-        first_banks = [ps.tile([P, 2, NQ], F32, name="turn2_first", tag=f"bank{2 + u}") for u in range(2)]
-        p_tags = {(1, 0): 4, (2, 0): 5, (1, 1): 6, (2, 1): 7}
+        sums = sb.tile([P, HALVES, PAGES], F32, name="sums")
         p_banks = {}
         for c in range(HALVES):
             for g in range(PAGES):
-                width = PAGE + 1 if g == PAGES - 1 else PAGE
-                prob = sb.tile([P, width], F32, name=f"prob{g}{c}")
+                prob = sb.tile([P, PAGE + 1 if g == LAST else PAGE], F32, name=f"prob{g}{c}")
                 nc.scalar.activation(
-                    prob[:], neg_s[g, c][:, 0:width], ACT.Exp, bias=mins[PAGES - 1, c][:], scale=-1.0,
+                    prob[:], neg_s[g, c], ACT.Exp, bias=mins[LAST, c][:], scale=-1.0,
                     accum_out=sums[:, c, g : g + 1],
                 )
-                if g > 0:
-                    p_banks[g, c] = ps.tile([P, PACK, P], F32, name="turn2", tag=f"bank{p_tags[g, c]}")
+                p_banks[g, c] = bank_tile([P, PACK, P], "p_turned", 2 + PAGES * c + g)
                 for t in range(PACK):
-                    if g == 0:
-                        dst = first_banks[t // 2][:, t % 2, c * P : (c + 1) * P]
-                    else:
-                        dst = p_banks[g, c][:, t, :]
-                    nc.tensor.transpose(dst, prob[:, t * P : (t + 1) * P], ident[:])
-        y_banks = [ps.tile([P, DV], F32, name=f"y{c}", tag=f"bank{c}") for c in range(HALVES)]
+                    nc.tensor.transpose(p_banks[g, c][:, t, :], prob[:, t * P : (t + 1) * P], ident[:])
+        y_banks = [bank_tile([P, DV], f"y{c}", c) for c in range(HALVES)]
 
-        steps = [(1, 0), (1, 1), (2, 0), (0, 0), (0, 1), (2, 1)]
-
-        w_planes = sb.tile([P, PACK, NQ], BF16, name="w_planes")
+        w_places = sb.tile([P, PACK, P], BF16, name="w_places")
         for t in range(PACK):
             nc.scalar.activation(
-                w_planes[:, t, :], first_banks[t // 2][:, t % 2, :], ACT.Copy, scale=vs_col[0][:, t : t + 1]
+                w_places[:, t, :], p_banks[0, 1][:, t, :], ACT.Copy, scale=vs_col[0][:, t : t + 1]
             )
-        nc.scalar.copy(
-            w_bf[:, 3:5].rearrange("p c q t -> p (c q) t"),
-            w_planes[:].rearrange("p t q -> p q t"),
-        )
+        w_scalar = sb.tile([P, 1, P, PACK], BF16, name="w_scalar", align_bytes=64)
+        nc.scalar.copy(w_scalar[:, 0], w_places[:].rearrange("p t m -> p m t"))
 
-        def weigh(i):
+        def weigh(dst, g, c):
             nc.vector.tensor_tensor(
-                w_bf[:, i],
-                p_banks[steps[i]][:].rearrange("p t q -> p q t"),
-                vs_col[steps[i][0]][:].unsqueeze(1).to_broadcast([P, P, PACK]),
+                dst,
+                p_banks[g, c][:].rearrange("p t m -> p m t"),
+                vs_col[g][:].unsqueeze(1).to_broadcast([P, P, PACK]),
                 ALU.mult,
             )
 
-        def multiply(lo, hi):
+        w_codes = sb.tile([P, HALVES * PAGES * P], U32, name="w_codes", align_bytes=64)
+        w_sc = sb.tile([P, HALVES * PAGES * P], U8, name="w_sc", align_bytes=64)
+        passes = []
+
+        def multiply(w, steps):
+            cols = slice(len(passes) * P, (len(passes) + len(steps)) * P)
             nc.vector.quantize_mx(
-                out=w_codes[:].rearrange("p i q -> p (i q)")[:, lo * P : hi * P].bitcast(FP8X4),
-                scales=w_sc[:].rearrange("p i q -> p (i q)")[:, lo * P : hi * P],
-                in_=w_bf[:].rearrange("p i q t -> p (i q t)")[:, lo * PAGE : hi * PAGE],
+                out=w_codes[:, cols].bitcast(FP8X4), scales=w_sc[:, cols], in_=w[:].rearrange("p i m t -> p (i m t)")
             )
-            for i in range(lo, hi):
-                g, c = steps[i]
+            for g, c in steps:
+                mine = slice(len(passes) * P, (len(passes) + 1) * P)
+                passes.append(c)
                 nc.tensor.matmul_mx(
                     out=y_banks[c][:],
-                    lhsT=w_codes[:, i, :].bitcast(FP8X4),
-                    lhsT_scale=w_sc[:, i, :],
+                    lhsT=w_codes[:, mine].bitcast(FP8X4),
+                    lhsT_scale=w_sc[:, mine],
                     rhs=vw[:, g * DV : (g + 1) * DV].bitcast(FP8X4),
                     rhs_scale=vsc[:, g * DV : (g + 1) * DV],
-                    start=(i < HALVES),
-                    stop=(i in (3, 5)),
+                    start=(passes.count(c) == 1),
+                    stop=(passes.count(c) == PAGES),
                 )
 
-        weigh(0)
-        weigh(1)
-        weigh(2)
-        multiply(0, 2)
+        total = sb.tile([P, HALVES], F32, name="total")
+        inv = sb.tile([P, HALVES], F32, name="inv")
+        w_first = sb.tile([P, 2, P, PACK], BF16, name="w_first", align_bytes=64)
+        w_second = sb.tile([P, 2, P, PACK], BF16, name="w_second", align_bytes=64)
+        w_third = sb.tile([P, 1, P, PACK], BF16, name="w_third", align_bytes=64)
+        weigh(w_first[:, 0], 0, 0)
+        weigh(w_first[:, 1], 1, 0)
+        weigh(w_second[:, 0], 2, 0)
+        multiply(w_first, [(0, 0), (1, 0)])
+        weigh(w_second[:, 1], 1, 1)
         nc.vector.tensor_reduce(total[:], sums[:], AX.X, ALU.add)
-        weigh(5)
+        weigh(w_third[:, 0], 2, 1)
         nc.vector.reciprocal(inv[:], total[:])
-        multiply(2, 4)
-        multiply(4, 6)
+        multiply(w_second, [(2, 0), (1, 1)])
+        multiply(w_third, [(2, 1)])
+        multiply(w_scalar, [(0, 1)])
 
+        y_sb = sb.tile([P, HALVES, DV], F32, name="y_sb")
         out_view = out[0].rearrange("(p c) e -> p c e", c=HALVES)
         for c in range(HALVES):
             nc.scalar.activation(y_sb[:, c, :], y_banks[c][:], ACT.Copy, scale=inv[:, c : c + 1])

@@ -26,10 +26,12 @@ QUADRANTS = 4
 LIST_COLS = PAGE // 16
 WORD = 4
 
-KW_AT = 0
-Q_RAW_AT = KW_AT + PAGE * WORD // 2
-MIN_AT = 8192
-MIN_COLS = 32
+Q_RAW_AT = 0
+KW1_AT = 4096
+START_AT = 8192
+MIN_AT = 16384
+MIN_COLS = PAGE + PAGES * DV + PAGES * DV // WORD
+POOL_PAGES = T // PAGE
 
 FLOPS = 2 * NQ * N * (D + DV)
 BYTES = D * NQ * 4 + T * (D + DV) + T * (D + DV) // 32 + 2 * T * 4 + NQ * 4 + P * (N + PAGES * DV) // 8 + NQ * DV * 4
@@ -54,47 +56,57 @@ def tile_attend_pkv8_soft_sink_kb_kernel(
         voffs_t = sb.tile([P, PAGES * DV // 16], U16, name="voffs_t")
         kw_pool = sb.tile([P, T], I32, name="kw_pool")
         ks_pool = sb.tile([P, T], U8, name="ks_pool")
-        vw_pool = sb.tile([P, T // PAGE * DV], I32, name="vw_pool")
         vsc_pool = sb.tile([P, T // PAGE * DV], U8, name="vsc_pool")
         kb_pool = sb.tile([P, T], F32, name="kb_pool")
-        vs_pool = sb.tile([P, T], F32, name="vs_pool")
-        vs_in = sb.tile([P, T // P], F32, name="vs_in")
+        vs_in = sb.tile([P, PAGE], F32, name="vs_in")
         sink_t = sb.tile([P, HALVES], F32, name="sink_t")
         ident = sb.tile([P, P], F32, name="ident")
         q_raw = reuse.tile([P, PACK, NQ], F32, name="q_raw", offset=Q_RAW_AT, align_bytes=64)
+        vw_pool = reuse.tile([P, T // PAGE * DV], I32, name="vw_pool", offset=Q_RAW_AT, align_bytes=64)
 
         nc.vector.memset(ks_pool[:].bitcast(I32), 0)
+        nc.vector.memset(vs_in[0 : P - POOL_PAGES, :], 0.0)
         nc.vector.memset(kb_pool[0:LIVE, :], 0.0)
+        nc.vector.memset(vsc_pool[:].bitcast(I32), 0)
         make_identity(nc, ident[:])
 
         nc.sync.dma_start(offs_t[:], offs)
         nc.sync.dma_start(kb_pool[LIVE:P, :], kb[0:1, :])
+        nc.sync.dma_start(vs_in[P - POOL_PAGES : P, :], vs[0].rearrange("(u j) -> u j", j=PAGE))
         for a in range(QUADRANTS):
             nc.scalar.dma_start(
                 ks_pool[32 * a : 32 * a + 4, :].bitcast(I32), k_scales[0, 4 * a : 4 * a + 4, :].bitcast(I32)
             )
-        nc.sync.dma_start(vs_in[:], vs[0].rearrange("(p c) -> p c", p=P))
-        nc.sync.dma_start(voffs_t[:], voffs)
-        nc.sync.dma_start(sink_t[:], sink[0].rearrange("(p c) o -> p (c o)", c=HALVES))
         nc.sync.dma_start(q_raw[:], qT[0].rearrange("(p j) q -> p j q", j=PACK))
         nc.sync.dma_start(kw_pool[:], k_words[0].rearrange("p t r -> p (t r)").bitcast(I32))
-        nc.sync.dma_start(
-            vw_pool[:].rearrange("p (u e) -> p u e", e=DV),
-            v_words.rearrange("u p e r -> p u (e r)").bitcast(I32),
-        )
-
-        vs_runs = vs_pool[:].rearrange("p (n a t) -> p a n t", n=P, t=PACK)
-        for a in range(T // P // PACK):
-            bank = bank_tile([P, PACK, P], "vs_bank", a % 4)
-            for t in range(PACK):
-                col = PACK * a + t
-                nc.tensor.transpose(bank[:, t, :], vs_in[:, col : col + 1].to_broadcast([P, P]), ident[:])
-            nc.scalar.activation(vs_runs[:, a], bank[:].rearrange("p t n -> p n t"), ACT.Copy)
+        nc.sync.dma_start(sink_t[:], sink[0].rearrange("(p c) o -> p (c o)", c=HALVES))
+        nc.sync.dma_start(voffs_t[:], voffs)
+        for a in range(QUADRANTS):
+            nc.sync.dma_start(
+                vsc_pool[32 * a : 32 * a + 4, :].bitcast(I32).rearrange("f (u e) -> f u e", e=DV // WORD),
+                v_scales[:, 4 * a : 4 * a + 4, :].rearrange("u f e -> f u e").bitcast(I32),
+            )
 
         q_bf = sb.tile([P, HALVES, P, PACK], BF16, name="q_bf", align_bytes=64)
         q_view = q_raw[:].rearrange("p j (m c) -> p c m j", c=HALVES)
         for c in range(HALVES):
             nc.scalar.copy(q_bf[:, c], q_view[:, c])
+        nc.sync.dma_start(
+            vw_pool[:].rearrange("p (u e) -> p u e", e=DV),
+            v_words.rearrange("u p e r -> p u (e r)").bitcast(I32),
+        )
+
+        vs_bank = bank_tile([P, PACK, P], "vs_bank", 7)
+        for t in range(PACK):
+            nc.tensor.transpose(vs_bank[:, t, :], vs_in[:, t:PAGE:PACK], ident[:])
+        vs_pool = sb.tile([P, T], F32, name="vs_pool")
+        for u in range(0, POOL_PAGES, 2):
+            first = P - POOL_PAGES + u
+            nc.scalar.activation(
+                vs_pool[:, u * PAGE : (u + 2) * PAGE].rearrange("p (u r t) -> p u r t", u=2, t=PACK),
+                vs_bank[:, :, first : first + 2].rearrange("p t u -> p u t").unsqueeze(2).to_broadcast([P, 2, P, PACK]),
+                ACT.Copy,
+            )
 
         kb_row = sb.tile([P, N], F32, name="kb_row")
         kb_col = []
@@ -107,37 +119,26 @@ def tile_attend_pkv8_soft_sink_kb_kernel(
             kb_col.append(sb.tile([P, PACK], F32, name=f"kb_col{g}"))
             nc.scalar.copy(kb_col[g][:], bank[:, :, LIVE])
 
-        ks = sb.tile([P, N], U8, name="ks", align_bytes=64)
-        nc.vector.tensor_copy(ks[:], ks_pool[:].indirect(offs_t[:]))
-
-        vs_col = [sb.tile([P, PACK], F32, name=f"vs_col{g}") for g in range(PAGES)]
-
-        def gather_vs(g, row):
-            nc.vector.tensor_copy(row[:], vs_pool[:].indirect(page_offs(g)))
-            nc.sync.dma_start(vs_col[g][:], row[LIVE:P, :])
-
-        for g in range(LAST):
-            gather_vs(g, sb.tile([P, PAGE], F32, name=f"vs_row{g}"))
+        kw = [
+            sb.tile([P, PAGE], U32, name="kw0", align_bytes=64),
+            reuse.tile([P, PAGE], U32, name="kw1", offset=KW1_AT, align_bytes=64),
+            sb.tile([P, PAGE], U32, name="kw2", align_bytes=64),
+        ]
+        ks = [sb.tile([P, PAGE], U8, name=f"ks{g}", align_bytes=64) for g in range(PAGES)]
+        for g in range(PAGES):
+            nc.vector.tensor_copy(ks[g][:], ks_pool[:].indirect(page_offs(g)))
 
         q_codes = sb.tile([P, NQ], U32, name="q_codes", align_bytes=64)
         q_sc = sb.tile([P, NQ], U8, name="q_sc", align_bytes=64)
         nc.vector.quantize_mx(
             out=q_codes[:].bitcast(FP8X4), scales=q_sc[:], in_=q_bf[:].rearrange("p c m j -> p (c m j)")
         )
-        nc.vector.memset(vsc_pool[:].bitcast(I32), 0)
-        for a in range(QUADRANTS):
-            nc.sync.dma_start(
-                vsc_pool[32 * a : 32 * a + 4, :].bitcast(I32).rearrange("f (u e) -> f u e", e=DV // WORD),
-                v_scales[:, 4 * a : 4 * a + 4, :].rearrange("u f e -> f u e").bitcast(I32),
-            )
 
         neg_s_last = sb.tile([P, HALVES, PAGE + 8], F32, name="neg_s_last")
-        nc.gpsimd.tensor_scalar(neg_s_last[:, :, PAGE], sink_t[:], -1.0, 0.0, ALU.mult, ALU.add)
+        nc.scalar.activation(neg_s_last[:, :, PAGE], sink_t[:], ACT.Copy, scale=-1.0)
+        first_start = reuse.tile([P, PAGE], F32, name="first_start", offset=START_AT, align_bytes=64)
+        nc.scalar.activation(first_start[:, 0:1], sink_t[:, 0:1], ACT.Copy, scale=-1.0)
 
-        kw = [
-            reuse.tile([P, PAGE], U32, name=f"kw{g}", offset=KW_AT + g * PAGE * WORD, align_bytes=64)
-            for g in range(PAGES)
-        ]
         s_turned = [sb.tile([P, PACK, NQ], F32, name=f"s_turned{g}") for g in range(PAGES)]
         score_banks = ((0, 1), (2, 3), (2, 3))
         turn_banks = ((4, 5), (6, 7), (0, 1))
@@ -152,7 +153,7 @@ def tile_attend_pkv8_soft_sink_kb_kernel(
                     nc.tensor.matmul_mx(
                         out=bank[:, jj, :],
                         lhsT=kw[g][:, j * P : (j + 1) * P].bitcast(FP8X4),
-                        lhsT_scale=ks[:, g * PAGE + j * P : g * PAGE + (j + 1) * P],
+                        lhsT_scale=ks[g][:, j * P : (j + 1) * P],
                         rhs=q_codes[:].bitcast(FP8X4),
                         rhs_scale=q_sc[:],
                         start=True,
@@ -178,12 +179,16 @@ def tile_attend_pkv8_soft_sink_kb_kernel(
             turn(g - 1)
         turn(LAST)
 
-        vs_row_last = reuse.tile([P, PAGE], F32, name="vs_row_last", offset=KW_AT + PAGE * WORD, align_bytes=64)
-        gather_vs(LAST, vs_row_last)
+        vs_page = [reuse.tile([P, PAGE], F32, name="vs_page0", offset=KW1_AT, align_bytes=64)]
+        nc.vector.tensor_copy(vs_page[0][:], vs_pool[:].indirect(page_offs(0)))
 
         neg_s = {}
         mins = {}
+        starts = (first_start[:, 0:1], neg_s_last[:, 1, PAGE : PAGE + 1])
         for g in range(PAGES):
+            if g == 1:
+                vs_page.append(reuse.tile([P, PAGE], F32, name="vs_page1", offset=START_AT, align_bytes=64))
+                nc.vector.tensor_copy(vs_page[1][:], vs_pool[:].indirect(page_offs(1)))
             for c in range(HALVES):
                 if g == LAST:
                     neg_s[g, c] = neg_s_last[:, c, 0 : PAGE + 1]
@@ -197,15 +202,17 @@ def tile_attend_pkv8_soft_sink_kb_kernel(
                     neg_s[g, c][:, 0:PAGE].rearrange("q (t z) -> q t z", t=PACK),
                     turned[g, c][:].rearrange("q (z t) -> q t z", t=PACK),
                     -1.0,
-                    neg_s_last[:, c, PAGE : PAGE + 1] if g == 0 else mins[g - 1, c][:, 0:1],
+                    starts[c] if g == 0 else mins[g - 1, c][:, 0:1],
                     ALU.mult,
                     ALU.min,
                     accum_out=mins[g, c][:, 0:1],
                 )
 
-        min_half = MIN_AT + MIN_COLS * WORD // 2
-        vw = reuse.tile([P, PAGES * DV], U32, name="vw", offset=min_half, align_bytes=64)
-        vsc = reuse.tile([P, PAGES * DV], U8, name="vsc", offset=min_half - PAGES * DV, align_bytes=64)
+        vs_page.append(reuse.tile([P, PAGE], F32, name="vs_page2", offset=MIN_AT, align_bytes=64))
+        nc.vector.tensor_copy(vs_page[LAST][:], vs_pool[:].indirect(page_offs(LAST)))
+        vw_at = MIN_AT + PAGE * WORD
+        vw = reuse.tile([P, PAGES * DV], U32, name="vw", offset=vw_at, align_bytes=64)
+        vsc = reuse.tile([P, PAGES * DV], U8, name="vsc", offset=vw_at + PAGES * DV * WORD, align_bytes=64)
         nc.vector.tensor_copy(vw[:], vw_pool[:].bitcast(U32).indirect(voffs_t[:]))
         nc.vector.tensor_copy(vsc[:], vsc_pool[:].indirect(voffs_t[:]))
 
@@ -223,60 +230,61 @@ def tile_attend_pkv8_soft_sink_kb_kernel(
                     nc.tensor.transpose(p_banks[g, c][:, t, :], prob[:, t * P : (t + 1) * P], ident[:])
         y_banks = [bank_tile([P, DV], f"y{c}", c) for c in range(HALVES)]
 
-        w_places = sb.tile([P, PACK, P], BF16, name="w_places")
-        for t in range(PACK):
-            nc.scalar.activation(
-                w_places[:, t, :], p_banks[0, 1][:, t, :], ACT.Copy, scale=vs_col[0][:, t : t + 1]
-            )
-        w_scalar = sb.tile([P, 1, P, PACK], BF16, name="w_scalar", align_bytes=64)
-        nc.scalar.copy(w_scalar[:, 0], w_places[:].rearrange("p t m -> p m t"))
+        w = {}
 
-        def weigh(dst, g, c):
+        def weigh_on_scalar(g, c):
+            places = sb.tile([P, PACK, P], BF16, name=f"w_places{g}{c}")
+            for t in range(PACK):
+                nc.scalar.activation(
+                    places[:, t, :], p_banks[g, c][:, t, :], ACT.Copy, scale=vs_page[g][:, t : t + 1]
+                )
+            w[g, c] = sb.tile([P, P, PACK], BF16, name=f"w{g}{c}", align_bytes=64)
+            nc.scalar.copy(w[g, c][:], places[:].rearrange("p t m -> p m t"))
+
+        def weigh_on_vector(g, c):
+            w[g, c] = sb.tile([P, P, PACK], BF16, name=f"w{g}{c}", align_bytes=64)
             nc.vector.tensor_tensor(
-                dst,
+                w[g, c][:],
                 p_banks[g, c][:].rearrange("p t m -> p m t"),
-                vs_col[g][:].unsqueeze(1).to_broadcast([P, P, PACK]),
+                vs_page[g][:].rearrange("p (m t) -> p m t", t=PACK),
                 ALU.mult,
             )
 
-        w_codes = sb.tile([P, HALVES * PAGES * P], U32, name="w_codes", align_bytes=64)
-        w_sc = sb.tile([P, HALVES * PAGES * P], U8, name="w_sc", align_bytes=64)
         passes = []
 
-        def multiply(w, steps):
-            cols = slice(len(passes) * P, (len(passes) + len(steps)) * P)
+        def multiply(g, c):
+            codes = sb.tile([P, P], U32, name=f"w_codes{g}{c}", align_bytes=64)
+            scales = sb.tile([P, P], U8, name=f"w_sc{g}{c}", align_bytes=64)
             nc.vector.quantize_mx(
-                out=w_codes[:, cols].bitcast(FP8X4), scales=w_sc[:, cols], in_=w[:].rearrange("p i m t -> p (i m t)")
+                out=codes[:].bitcast(FP8X4), scales=scales[:], in_=w[g, c][:].rearrange("p m t -> p (m t)")
             )
-            for g, c in steps:
-                mine = slice(len(passes) * P, (len(passes) + 1) * P)
-                passes.append(c)
-                nc.tensor.matmul_mx(
-                    out=y_banks[c][:],
-                    lhsT=w_codes[:, mine].bitcast(FP8X4),
-                    lhsT_scale=w_sc[:, mine],
-                    rhs=vw[:, g * DV : (g + 1) * DV].bitcast(FP8X4),
-                    rhs_scale=vsc[:, g * DV : (g + 1) * DV],
-                    start=(passes.count(c) == 1),
-                    stop=(passes.count(c) == PAGES),
-                )
+            passes.append(c)
+            nc.tensor.matmul_mx(
+                out=y_banks[c][:],
+                lhsT=codes[:].bitcast(FP8X4),
+                lhsT_scale=scales[:],
+                rhs=vw[:, g * DV : (g + 1) * DV].bitcast(FP8X4),
+                rhs_scale=vsc[:, g * DV : (g + 1) * DV],
+                start=(passes.count(c) == 1),
+                stop=(passes.count(c) == PAGES),
+            )
 
         total = sb.tile([P, HALVES], F32, name="total")
         inv = sb.tile([P, HALVES], F32, name="inv")
-        w_first = sb.tile([P, 2, P, PACK], BF16, name="w_first", align_bytes=64)
-        w_second = sb.tile([P, 2, P, PACK], BF16, name="w_second", align_bytes=64)
-        w_third = sb.tile([P, 1, P, PACK], BF16, name="w_third", align_bytes=64)
-        weigh(w_first[:, 0], 0, 0)
-        weigh(w_first[:, 1], 1, 0)
-        weigh(w_second[:, 0], 2, 0)
-        multiply(w_first, [(0, 0), (1, 0)])
-        weigh(w_second[:, 1], 1, 1)
+        weigh_on_scalar(0, 0)
+        weigh_on_scalar(0, 1)
         nc.vector.tensor_reduce(total[:], sums[:], AX.X, ALU.add)
-        weigh(w_third[:, 0], 2, 1)
+        weigh_on_vector(1, 0)
         nc.vector.reciprocal(inv[:], total[:])
-        multiply(w_second, [(2, 0), (1, 1)])
-        multiply(w_third, [(2, 1)])
-        multiply(w_scalar, [(0, 1)])
+        weigh_on_vector(2, 0)
+        multiply(1, 0)
+        multiply(0, 0)
+        weigh_on_vector(1, 1)
+        multiply(2, 0)
+        weigh_on_vector(2, 1)
+        multiply(1, 1)
+        multiply(0, 1)
+        multiply(2, 1)
 
         y_sb = sb.tile([P, HALVES, DV], F32, name="y_sb")
         out_view = out[0].rearrange("(p c) e -> p c e", c=HALVES)

@@ -27,10 +27,9 @@ LIST_COLS = PAGE // 16
 WORD = 4
 
 Q_RAW_AT = 0
-KW1_AT = 4096
-START_AT = 8192
+KW0_AT = 4096
 MIN_AT = 16384
-MIN_COLS = PAGE + PAGES * DV + PAGES * DV // WORD
+MIN_COLS = LAST * PAGE + PAGES * DV + PAGES * DV // WORD
 POOL_PAGES = T // PAGE
 
 FLOPS = 2 * NQ * N * (D + DV)
@@ -120,13 +119,12 @@ def tile_attend_pkv8_soft_sink_kb_kernel(
             nc.scalar.copy(kb_col[g][:], bank[:, :, LIVE])
 
         kw = [
-            sb.tile([P, PAGE], U32, name="kw0", align_bytes=64),
-            reuse.tile([P, PAGE], U32, name="kw1", offset=KW1_AT, align_bytes=64),
+            reuse.tile([P, PAGE], U32, name="kw0", offset=KW0_AT, align_bytes=64),
+            sb.tile([P, PAGE], U32, name="kw1", align_bytes=64),
             sb.tile([P, PAGE], U32, name="kw2", align_bytes=64),
         ]
-        ks = [sb.tile([P, PAGE], U8, name=f"ks{g}", align_bytes=64) for g in range(PAGES)]
-        for g in range(PAGES):
-            nc.vector.tensor_copy(ks[g][:], ks_pool[:].indirect(page_offs(g)))
+        ks = sb.tile([P, N], U8, name="ks", align_bytes=64)
+        nc.vector.tensor_copy(ks[:], ks_pool[:].indirect(offs_t[:]))
 
         q_codes = sb.tile([P, NQ], U32, name="q_codes", align_bytes=64)
         q_sc = sb.tile([P, NQ], U8, name="q_sc", align_bytes=64)
@@ -134,14 +132,24 @@ def tile_attend_pkv8_soft_sink_kb_kernel(
             out=q_codes[:].bitcast(FP8X4), scales=q_sc[:], in_=q_bf[:].rearrange("p c m j -> p (c m j)")
         )
 
+        warm = bank_tile([P, NQ], "warm", 3)
+        for repeat in range(3):
+            nc.tensor.matmul_mx(
+                out=warm[:],
+                lhsT=q_codes[:, 0:P].bitcast(FP8X4),
+                lhsT_scale=q_sc[:, 0:P],
+                rhs=q_codes[:].bitcast(FP8X4),
+                rhs_scale=q_sc[:],
+                start=True,
+                stop=True,
+            )
+
         neg_s_last = sb.tile([P, HALVES, PAGE + 8], F32, name="neg_s_last")
         nc.scalar.activation(neg_s_last[:, :, PAGE], sink_t[:], ACT.Copy, scale=-1.0)
-        first_start = reuse.tile([P, PAGE], F32, name="first_start", offset=START_AT, align_bytes=64)
-        nc.scalar.activation(first_start[:, 0:1], sink_t[:, 0:1], ACT.Copy, scale=-1.0)
 
         s_turned = [sb.tile([P, PACK, NQ], F32, name=f"s_turned{g}") for g in range(PAGES)]
-        score_banks = ((0, 1), (2, 3), (2, 3))
-        turn_banks = ((4, 5), (6, 7), (0, 1))
+        score_banks = ((0, 1), (2, 3), (0, 1))
+        turn_banks = ((4, 5), (6, 7), (2, 3))
         turned = {}
 
         def scores(g):
@@ -153,7 +161,7 @@ def tile_attend_pkv8_soft_sink_kb_kernel(
                     nc.tensor.matmul_mx(
                         out=bank[:, jj, :],
                         lhsT=kw[g][:, j * P : (j + 1) * P].bitcast(FP8X4),
-                        lhsT_scale=ks[g][:, j * P : (j + 1) * P],
+                        lhsT_scale=ks[:, g * PAGE + j * P : g * PAGE + (j + 1) * P],
                         rhs=q_codes[:].bitcast(FP8X4),
                         rhs_scale=q_sc[:],
                         start=True,
@@ -179,16 +187,12 @@ def tile_attend_pkv8_soft_sink_kb_kernel(
             turn(g - 1)
         turn(LAST)
 
-        vs_page = [reuse.tile([P, PAGE], F32, name="vs_page0", offset=KW1_AT, align_bytes=64)]
-        nc.vector.tensor_copy(vs_page[0][:], vs_pool[:].indirect(page_offs(0)))
+        vs_page = [reuse.tile([P, PAGE], F32, name="vs_page0", offset=KW0_AT, align_bytes=64)[:]]
+        nc.vector.tensor_copy(vs_page[0], vs_pool[:].indirect(page_offs(0)))
 
         neg_s = {}
         mins = {}
-        starts = (first_start[:, 0:1], neg_s_last[:, 1, PAGE : PAGE + 1])
         for g in range(PAGES):
-            if g == 1:
-                vs_page.append(reuse.tile([P, PAGE], F32, name="vs_page1", offset=START_AT, align_bytes=64))
-                nc.vector.tensor_copy(vs_page[1][:], vs_pool[:].indirect(page_offs(1)))
             for c in range(HALVES):
                 if g == LAST:
                     neg_s[g, c] = neg_s_last[:, c, 0 : PAGE + 1]
@@ -202,15 +206,16 @@ def tile_attend_pkv8_soft_sink_kb_kernel(
                     neg_s[g, c][:, 0:PAGE].rearrange("q (t z) -> q t z", t=PACK),
                     turned[g, c][:].rearrange("q (z t) -> q t z", t=PACK),
                     -1.0,
-                    starts[c] if g == 0 else mins[g - 1, c][:, 0:1],
+                    neg_s_last[:, c, PAGE : PAGE + 1] if g == 0 else mins[g - 1, c][:, 0:1],
                     ALU.mult,
                     ALU.min,
                     accum_out=mins[g, c][:, 0:1],
                 )
 
-        vs_page.append(reuse.tile([P, PAGE], F32, name="vs_page2", offset=MIN_AT, align_bytes=64))
-        nc.vector.tensor_copy(vs_page[LAST][:], vs_pool[:].indirect(page_offs(LAST)))
-        vw_at = MIN_AT + PAGE * WORD
+        vs_rest = reuse.tile([P, LAST * PAGE], F32, name="vs_rest", offset=MIN_AT, align_bytes=64)
+        nc.vector.tensor_copy(vs_rest[:], vs_pool[:].indirect(offs_t[:, LIST_COLS:]))
+        vs_page.extend(vs_rest[:, (g - 1) * PAGE : g * PAGE] for g in range(1, PAGES))
+        vw_at = MIN_AT + LAST * PAGE * WORD
         vw = reuse.tile([P, PAGES * DV], U32, name="vw", offset=vw_at, align_bytes=64)
         vsc = reuse.tile([P, PAGES * DV], U8, name="vsc", offset=vw_at + PAGES * DV * WORD, align_bytes=64)
         nc.vector.tensor_copy(vw[:], vw_pool[:].bitcast(U32).indirect(voffs_t[:]))
@@ -218,6 +223,7 @@ def tile_attend_pkv8_soft_sink_kb_kernel(
 
         sums = sb.tile([P, HALVES, PAGES], F32, name="sums")
         p_banks = {}
+        wide = [bank_tile([P, 2, NQ], "p_wide", pair) for pair in range(2)]
         for c in range(HALVES):
             for g in range(PAGES):
                 prob = sb.tile([P, PAGE + 1 if g == LAST else PAGE], F32, name=f"prob{g}{c}")
@@ -225,28 +231,28 @@ def tile_attend_pkv8_soft_sink_kb_kernel(
                     prob[:], neg_s[g, c], ACT.Exp, bias=mins[LAST, c][:], scale=-1.0,
                     accum_out=sums[:, c, g : g + 1],
                 )
-                p_banks[g, c] = bank_tile([P, PACK, P], "p_turned", 2 + PAGES * c + g)
+                if g > 0:
+                    p_banks[g, c] = bank_tile([P, PACK, P], "p_turned", ((4, 5), (6, 7))[c][g - 1])
                 for t in range(PACK):
-                    nc.tensor.transpose(p_banks[g, c][:, t, :], prob[:, t * P : (t + 1) * P], ident[:])
-        y_banks = [bank_tile([P, DV], f"y{c}", c) for c in range(HALVES)]
+                    dst = wide[t // 2][:, t % 2, c * P : (c + 1) * P] if g == 0 else p_banks[g, c][:, t, :]
+                    nc.tensor.transpose(dst, prob[:, t * P : (t + 1) * P], ident[:])
+        y_banks = [bank_tile([P, DV], f"y{c}", 2 + c) for c in range(HALVES)]
 
         w = {}
 
-        def weigh_on_scalar(g, c):
-            places = sb.tile([P, PACK, P], BF16, name=f"w_places{g}{c}")
-            for t in range(PACK):
-                nc.scalar.activation(
-                    places[:, t, :], p_banks[g, c][:, t, :], ACT.Copy, scale=vs_page[g][:, t : t + 1]
-                )
-            w[g, c] = sb.tile([P, P, PACK], BF16, name=f"w{g}{c}", align_bytes=64)
-            nc.scalar.copy(w[g, c][:], places[:].rearrange("p t m -> p m t"))
+        places = sb.tile([P, PACK, NQ], BF16, name="places")
+        for t in range(PACK):
+            nc.scalar.activation(places[:, t, :], wide[t // 2][:, t % 2, :], ACT.Copy, scale=vs_page[0][:, t : t + 1])
+        for c in range(HALVES):
+            w[0, c] = sb.tile([P, P, PACK], BF16, name=f"w0{c}", align_bytes=64)
+            nc.scalar.copy(w[0, c][:], places[:, :, c * P : (c + 1) * P].rearrange("p t m -> p m t"))
 
         def weigh_on_vector(g, c):
             w[g, c] = sb.tile([P, P, PACK], BF16, name=f"w{g}{c}", align_bytes=64)
             nc.vector.tensor_tensor(
                 w[g, c][:],
                 p_banks[g, c][:].rearrange("p t m -> p m t"),
-                vs_page[g][:].rearrange("p (m t) -> p m t", t=PACK),
+                vs_page[g].rearrange("p (m t) -> p m t", t=PACK),
                 ALU.mult,
             )
 
@@ -271,16 +277,14 @@ def tile_attend_pkv8_soft_sink_kb_kernel(
 
         total = sb.tile([P, HALVES], F32, name="total")
         inv = sb.tile([P, HALVES], F32, name="inv")
-        weigh_on_scalar(0, 0)
-        weigh_on_scalar(0, 1)
-        nc.vector.tensor_reduce(total[:], sums[:], AX.X, ALU.add)
         weigh_on_vector(1, 0)
-        nc.vector.reciprocal(inv[:], total[:])
+        nc.vector.tensor_reduce(total[:], sums[:], AX.X, ALU.add)
         weigh_on_vector(2, 0)
+        nc.vector.reciprocal(inv[:], total[:])
         multiply(1, 0)
-        multiply(0, 0)
         weigh_on_vector(1, 1)
         multiply(2, 0)
+        multiply(0, 0)
         weigh_on_vector(2, 1)
         multiply(1, 1)
         multiply(0, 1)

@@ -21,16 +21,19 @@ PAGE = 512
 PAGES = N // PAGE
 HALVES = NQ // P
 LAST = PAGES - 1
+POOL_PAGES = T // PAGE
 LIVE = P - 1
+VS_ROW0 = P - POOL_PAGES
 QUADRANTS = 4
 LIST_COLS = PAGE // 16
 WORD = 4
+
+PAGES_A_COPY = 2
 
 Q_RAW_AT = 0
 KW0_AT = 4096
 MIN_AT = 16384
 MIN_COLS = LAST * PAGE + PAGES * DV + PAGES * DV // WORD
-POOL_PAGES = T // PAGE
 
 FLOPS = 2 * NQ * N * (D + DV)
 BYTES = D * NQ * 4 + T * (D + DV) + T * (D + DV) // 32 + 2 * T * 4 + NQ * 4 + P * (N + PAGES * DV) // 8 + NQ * DV * 4
@@ -64,14 +67,14 @@ def tile_attend_pkv8_soft_sink_kb_kernel(
         vw_pool = reuse.tile([P, T // PAGE * DV], I32, name="vw_pool", offset=Q_RAW_AT, align_bytes=64)
 
         nc.vector.memset(ks_pool[:].bitcast(I32), 0)
-        nc.vector.memset(vs_in[0 : P - POOL_PAGES, :], 0.0)
+        nc.vector.memset(vs_in[0:VS_ROW0, :], 0.0)
         nc.vector.memset(kb_pool[0:LIVE, :], 0.0)
         nc.vector.memset(vsc_pool[:].bitcast(I32), 0)
         make_identity(nc, ident[:])
 
         nc.sync.dma_start(offs_t[:], offs)
         nc.sync.dma_start(kb_pool[LIVE:P, :], kb[0:1, :])
-        nc.sync.dma_start(vs_in[P - POOL_PAGES : P, :], vs[0].rearrange("(u j) -> u j", j=PAGE))
+        nc.sync.dma_start(vs_in[VS_ROW0:P, :], vs[0].rearrange("(u j) -> u j", j=PAGE))
         for a in range(QUADRANTS):
             nc.scalar.dma_start(
                 ks_pool[32 * a : 32 * a + 4, :].bitcast(I32), k_scales[0, 4 * a : 4 * a + 4, :].bitcast(I32)
@@ -90,6 +93,7 @@ def tile_attend_pkv8_soft_sink_kb_kernel(
         q_view = q_raw[:].rearrange("p j (m c) -> p c m j", c=HALVES)
         for c in range(HALVES):
             nc.scalar.copy(q_bf[:, c], q_view[:, c])
+
         nc.sync.dma_start(
             vw_pool[:].rearrange("p (u e) -> p u e", e=DV),
             v_words.rearrange("u p e r -> p u (e r)").bitcast(I32),
@@ -99,11 +103,13 @@ def tile_attend_pkv8_soft_sink_kb_kernel(
         for t in range(PACK):
             nc.tensor.transpose(vs_bank[:, t, :], vs_in[:, t:PAGE:PACK], ident[:])
         vs_pool = sb.tile([P, T], F32, name="vs_pool")
-        for u in range(0, POOL_PAGES, 2):
-            first = P - POOL_PAGES + u
+        for u in range(0, POOL_PAGES, PAGES_A_COPY):
+            by_page = vs_bank[:, :, VS_ROW0 + u : VS_ROW0 + u + PAGES_A_COPY].rearrange("p t u -> p u t")
             nc.scalar.activation(
-                vs_pool[:, u * PAGE : (u + 2) * PAGE].rearrange("p (u r t) -> p u r t", u=2, t=PACK),
-                vs_bank[:, :, first : first + 2].rearrange("p t u -> p u t").unsqueeze(2).to_broadcast([P, 2, P, PACK]),
+                vs_pool[:, u * PAGE : (u + PAGES_A_COPY) * PAGE].rearrange(
+                    "p (u r t) -> p u r t", u=PAGES_A_COPY, t=PACK
+                ),
+                by_page.unsqueeze(2).to_broadcast([P, PAGES_A_COPY, P, PACK]),
                 ACT.Copy,
             )
 
@@ -131,18 +137,6 @@ def tile_attend_pkv8_soft_sink_kb_kernel(
         nc.vector.quantize_mx(
             out=q_codes[:].bitcast(FP8X4), scales=q_sc[:], in_=q_bf[:].rearrange("p c m j -> p (c m j)")
         )
-
-        warm = bank_tile([P, NQ], "warm", 3)
-        for repeat in range(3):
-            nc.tensor.matmul_mx(
-                out=warm[:],
-                lhsT=q_codes[:, 0:P].bitcast(FP8X4),
-                lhsT_scale=q_sc[:, 0:P],
-                rhs=q_codes[:].bitcast(FP8X4),
-                rhs_scale=q_sc[:],
-                start=True,
-                stop=True,
-            )
 
         neg_s_last = sb.tile([P, HALVES, PAGE + 8], F32, name="neg_s_last")
         nc.scalar.activation(neg_s_last[:, :, PAGE], sink_t[:], ACT.Copy, scale=-1.0)
@@ -223,7 +217,7 @@ def tile_attend_pkv8_soft_sink_kb_kernel(
 
         sums = sb.tile([P, HALVES, PAGES], F32, name="sums")
         p_banks = {}
-        wide = [bank_tile([P, 2, NQ], "p_wide", pair) for pair in range(2)]
+        wide = [bank_tile([P, 2, NQ], "p_wide", pair) for pair in range(PACK // 2)]
         for c in range(HALVES):
             for g in range(PAGES):
                 prob = sb.tile([P, PAGE + 1 if g == LAST else PAGE], F32, name=f"prob{g}{c}")
@@ -232,14 +226,13 @@ def tile_attend_pkv8_soft_sink_kb_kernel(
                     accum_out=sums[:, c, g : g + 1],
                 )
                 if g > 0:
-                    p_banks[g, c] = bank_tile([P, PACK, P], "p_turned", ((4, 5), (6, 7))[c][g - 1])
+                    p_banks[g, c] = bank_tile([P, PACK, P], "p_turned", 4 + LAST * c + g - 1)
                 for t in range(PACK):
                     dst = wide[t // 2][:, t % 2, c * P : (c + 1) * P] if g == 0 else p_banks[g, c][:, t, :]
                     nc.tensor.transpose(dst, prob[:, t * P : (t + 1) * P], ident[:])
         y_banks = [bank_tile([P, DV], f"y{c}", 2 + c) for c in range(HALVES)]
 
         w = {}
-
         places = sb.tile([P, PACK, NQ], BF16, name="places")
         for t in range(PACK):
             nc.scalar.activation(places[:, t, :], wide[t // 2][:, t % 2, :], ACT.Copy, scale=vs_page[0][:, t : t + 1])

@@ -28,12 +28,12 @@ QUADRANTS = 4
 LIST_COLS = PAGE // 16
 WORD = 4
 
-PAGES_A_COPY = 2
-
 Q_RAW_AT = 0
 KW0_AT = 4096
+KB_COL_AT = 8192
 MIN_AT = 16384
-MIN_COLS = LAST * PAGE + PAGES * DV + PAGES * DV // WORD
+VS_SMALL_AT = 32768
+MIN_COLS = PAGE + PAGES * DV + PAGES * DV // WORD
 
 FLOPS = 2 * NQ * N * (D + DV)
 BYTES = D * NQ * 4 + T * (D + DV) + T * (D + DV) // 32 + 2 * T * 4 + NQ * 4 + P * (N + PAGES * DV) // 8 + NQ * DV * 4
@@ -73,13 +73,13 @@ def tile_attend_pkv8_soft_sink_kb_kernel(
         make_identity(nc, ident[:])
 
         nc.sync.dma_start(offs_t[:], offs)
-        nc.sync.dma_start(kb_pool[LIVE:P, :], kb[0:1, :])
         nc.sync.dma_start(vs_in[VS_ROW0:P, :], vs[0].rearrange("(u j) -> u j", j=PAGE))
+        nc.sync.dma_start(q_raw[:], qT[0].rearrange("(p j) q -> p j q", j=PACK))
+        nc.sync.dma_start(kb_pool[LIVE:P, :], kb[0:1, :])
         for a in range(QUADRANTS):
-            nc.scalar.dma_start(
+            nc.sync.dma_start(
                 ks_pool[32 * a : 32 * a + 4, :].bitcast(I32), k_scales[0, 4 * a : 4 * a + 4, :].bitcast(I32)
             )
-        nc.sync.dma_start(q_raw[:], qT[0].rearrange("(p j) q -> p j q", j=PACK))
         nc.sync.dma_start(kw_pool[:], k_words[0].rearrange("p t r -> p (t r)").bitcast(I32))
         nc.sync.dma_start(sink_t[:], sink[0].rearrange("(p c) o -> p (c o)", c=HALVES))
         nc.sync.dma_start(voffs_t[:], voffs)
@@ -92,7 +92,7 @@ def tile_attend_pkv8_soft_sink_kb_kernel(
         q_bf = sb.tile([P, HALVES, P, PACK], BF16, name="q_bf", align_bytes=64)
         q_view = q_raw[:].rearrange("p j (m c) -> p c m j", c=HALVES)
         for c in range(HALVES):
-            nc.scalar.copy(q_bf[:, c], q_view[:, c])
+            nc.scalar.activation(q_bf[:, c], q_view[:, c], ACT.Copy)
 
         nc.sync.dma_start(
             vw_pool[:].rearrange("p (u e) -> p u e", e=DV),
@@ -102,34 +102,31 @@ def tile_attend_pkv8_soft_sink_kb_kernel(
         vs_bank = bank_tile([P, PACK, P], "vs_bank", 7)
         for t in range(PACK):
             nc.tensor.transpose(vs_bank[:, t, :], vs_in[:, t:PAGE:PACK], ident[:])
-        vs_pool = sb.tile([P, T], F32, name="vs_pool")
-        for u in range(0, POOL_PAGES, PAGES_A_COPY):
-            by_page = vs_bank[:, :, VS_ROW0 + u : VS_ROW0 + u + PAGES_A_COPY].rearrange("p t u -> p u t")
-            nc.scalar.activation(
-                vs_pool[:, u * PAGE : (u + PAGES_A_COPY) * PAGE].rearrange(
-                    "p (u r t) -> p u r t", u=PAGES_A_COPY, t=PACK
-                ),
-                by_page.unsqueeze(2).to_broadcast([P, PAGES_A_COPY, P, PACK]),
-                ACT.Copy,
-            )
+        vs_small = reuse.tile([P, POOL_PAGES, PACK], F32, name="vs_small", offset=VS_SMALL_AT, align_bytes=64)
+        nc.vector.tensor_copy(vs_small[:], vs_bank[:, :, VS_ROW0:P].rearrange("p t u -> p u t"))
 
-        kb_row = sb.tile([P, N], F32, name="kb_row")
-        kb_col = []
+        vs_pool = sb.tile([P, T], F32, name="vs_pool")
+        nc.vector.tensor_copy(
+            vs_pool[:].rearrange("p (u r t) -> p u r t", u=POOL_PAGES, t=PACK),
+            vs_small[:].unsqueeze(2).to_broadcast([P, POOL_PAGES, P, PACK]),
+        )
+
+        kb_bank = bank_tile([P, P + 2 * PAGES * PACK], "kb_bank", 6)
         for g in range(PAGES):
-            nc.vector.tensor_copy(kb_row[:, g * PAGE : (g + 1) * PAGE], kb_pool[:].indirect(page_offs(g)))
-            bank = bank_tile([P, PACK, P], "kb_bank", 4 + g)
-            for j in range(PACK):
-                first = g * PAGE + j * P
-                nc.tensor.transpose(bank[:, j, :], kb_row[:, first : first + P], ident[:])
-            kb_col.append(sb.tile([P, PACK], F32, name=f"kb_col{g}"))
-            nc.scalar.copy(kb_col[g][:], bank[:, :, LIVE])
+            kb_row = sb.tile([P, PAGE], F32, name=f"kb_row{g}")
+            nc.scalar.activation(kb_row[:], kb_pool[:].indirect(page_offs(g)), ACT.Copy)
+            for j in reversed(range(PACK)):
+                at = 2 * ((LAST - g) * PACK + j)
+                nc.tensor.transpose(kb_bank[:, at : at + P], kb_row[:, j * P : (j + 1) * P], ident[:])
+        kb_col = reuse.tile([P, PAGES * PACK], F32, name="kb_col", offset=KB_COL_AT, align_bytes=64)
+        nc.scalar.copy(kb_col[:], kb_bank[:, LIVE : LIVE + 2 * PAGES * PACK : 2])
 
         kw = [
             reuse.tile([P, PAGE], U32, name="kw0", offset=KW0_AT, align_bytes=64),
             sb.tile([P, PAGE], U32, name="kw1", align_bytes=64),
             sb.tile([P, PAGE], U32, name="kw2", align_bytes=64),
         ]
-        ks = sb.tile([P, N], U8, name="ks", align_bytes=64)
+        ks = reuse.tile([P, N], U8, name="ks", offset=VS_SMALL_AT, align_bytes=64)
         nc.vector.tensor_copy(ks[:], ks_pool[:].indirect(offs_t[:]))
 
         q_codes = sb.tile([P, NQ], U32, name="q_codes", align_bytes=64)
@@ -139,7 +136,7 @@ def tile_attend_pkv8_soft_sink_kb_kernel(
         )
 
         neg_s_last = sb.tile([P, HALVES, PAGE + 8], F32, name="neg_s_last")
-        nc.scalar.activation(neg_s_last[:, :, PAGE], sink_t[:], ACT.Copy, scale=-1.0)
+        nc.gpsimd.tensor_scalar(neg_s_last[:, :, PAGE], sink_t[:], -1.0, 0.0, ALU.mult, ALU.add)
 
         s_turned = [sb.tile([P, PACK, NQ], F32, name=f"s_turned{g}") for g in range(PAGES)]
         score_banks = ((0, 1), (2, 3), (0, 1))
@@ -164,7 +161,7 @@ def tile_attend_pkv8_soft_sink_kb_kernel(
                 for jj in range(2):
                     j = 2 * pair + jj
                     nc.scalar.activation(
-                        s_turned[g][:, j, :], bank[:, jj, :], ACT.Identity, bias=kb_col[g][:, j : j + 1]
+                        s_turned[g][:, j, :], bank[:, jj, :], ACT.Identity, bias=kb_col[:, (LAST - g) * PACK + j : (LAST - g) * PACK + j + 1]
                     )
 
         def turn(g):
@@ -181,8 +178,12 @@ def tile_attend_pkv8_soft_sink_kb_kernel(
             turn(g - 1)
         turn(LAST)
 
-        vs_page = [reuse.tile([P, PAGE], F32, name="vs_page0", offset=KW0_AT, align_bytes=64)[:]]
-        nc.vector.tensor_copy(vs_page[0], vs_pool[:].indirect(page_offs(0)))
+        vs_page = [
+            reuse.tile([P, PAGE], F32, name="vs_page0", offset=KB_COL_AT, align_bytes=64)[:],
+            reuse.tile([P, PAGE], F32, name="vs_page1", offset=KW0_AT, align_bytes=64)[:],
+        ]
+        nc.vector.tensor_copy(vs_page[1], vs_pool[:].indirect(page_offs(1)))
+        nc.scalar.activation(vs_page[0], vs_pool[:].indirect(page_offs(0)), ACT.Copy)
 
         neg_s = {}
         mins = {}
@@ -206,10 +207,9 @@ def tile_attend_pkv8_soft_sink_kb_kernel(
                     accum_out=mins[g, c][:, 0:1],
                 )
 
-        vs_rest = reuse.tile([P, LAST * PAGE], F32, name="vs_rest", offset=MIN_AT, align_bytes=64)
-        nc.vector.tensor_copy(vs_rest[:], vs_pool[:].indirect(offs_t[:, LIST_COLS:]))
-        vs_page.extend(vs_rest[:, (g - 1) * PAGE : g * PAGE] for g in range(1, PAGES))
-        vw_at = MIN_AT + LAST * PAGE * WORD
+        vs_page.append(reuse.tile([P, PAGE], F32, name="vs_page2", offset=MIN_AT, align_bytes=64)[:])
+        nc.vector.tensor_copy(vs_page[LAST], vs_pool[:].indirect(page_offs(LAST)))
+        vw_at = MIN_AT + PAGE * WORD
         vw = reuse.tile([P, PAGES * DV], U32, name="vw", offset=vw_at, align_bytes=64)
         vsc = reuse.tile([P, PAGES * DV], U8, name="vsc", offset=vw_at + PAGES * DV * WORD, align_bytes=64)
         nc.vector.tensor_copy(vw[:], vw_pool[:].bitcast(U32).indirect(voffs_t[:]))

@@ -30,10 +30,13 @@ WORD = 4
 
 Q_RAW_AT = 0
 KW0_AT = 4096
+KW1_AT = 6144
 KB_COL_AT = 8192
 MIN_AT = 16384
 VS_SMALL_AT = 32768
-MIN_COLS = PAGE + PAGES * DV + PAGES * DV // WORD
+MIN_COLS = PAGES * DV + PAGES * DV // WORD
+
+P_BANKS = (0, 1, 4, 5, 6, 7)
 
 FLOPS = 2 * NQ * N * (D + DV)
 BYTES = D * NQ * 4 + T * (D + DV) + T * (D + DV) // 32 + 2 * T * 4 + NQ * 4 + P * (N + PAGES * DV) // 8 + NQ * DV * 4
@@ -74,10 +77,10 @@ def tile_attend_pkv8_soft_sink_kb_kernel(
 
         nc.sync.dma_start(offs_t[:], offs)
         nc.sync.dma_start(vs_in[VS_ROW0:P, :], vs[0].rearrange("(u j) -> u j", j=PAGE))
-        nc.sync.dma_start(q_raw[:], qT[0].rearrange("(p j) q -> p j q", j=PACK))
         nc.sync.dma_start(kb_pool[LIVE:P, :], kb[0:1, :])
+        nc.sync.dma_start(q_raw[:], qT[0].rearrange("(p j) q -> p j q", j=PACK))
         for a in range(QUADRANTS):
-            nc.sync.dma_start(
+            nc.scalar.dma_start(
                 ks_pool[32 * a : 32 * a + 4, :].bitcast(I32), k_scales[0, 4 * a : 4 * a + 4, :].bitcast(I32)
             )
         nc.sync.dma_start(kw_pool[:], k_words[0].rearrange("p t r -> p (t r)").bitcast(I32))
@@ -111,6 +114,9 @@ def tile_attend_pkv8_soft_sink_kb_kernel(
             vs_small[:].unsqueeze(2).to_broadcast([P, POOL_PAGES, P, PACK]),
         )
 
+        vs_page = {1: sb.tile([P, PAGE], F32, name="vs_page1")[:]}
+        nc.vector.tensor_copy(vs_page[1], vs_pool[:].indirect(page_offs(1)))
+
         kb_bank = bank_tile([P, P + 2 * PAGES * PACK], "kb_bank", 6)
         for g in range(PAGES):
             kb_row = sb.tile([P, PAGE], F32, name=f"kb_row{g}")
@@ -123,11 +129,12 @@ def tile_attend_pkv8_soft_sink_kb_kernel(
 
         kw = [
             reuse.tile([P, PAGE], U32, name="kw0", offset=KW0_AT, align_bytes=64),
-            sb.tile([P, PAGE], U32, name="kw1", align_bytes=64),
+            reuse.tile([P, PAGE], U32, name="kw1", offset=KW1_AT, align_bytes=64),
             sb.tile([P, PAGE], U32, name="kw2", align_bytes=64),
         ]
-        ks = reuse.tile([P, N], U8, name="ks", offset=VS_SMALL_AT, align_bytes=64)
-        nc.vector.tensor_copy(ks[:], ks_pool[:].indirect(offs_t[:]))
+        ks_early = reuse.tile([P, LAST * PAGE], U8, name="ks_early", offset=VS_SMALL_AT, align_bytes=64)
+        nc.vector.tensor_copy(ks_early[:], ks_pool[:].indirect(offs_t[:, 0 : LAST * LIST_COLS]))
+        ks = [ks_early[:, g * PAGE : (g + 1) * PAGE] for g in range(LAST)]
 
         q_codes = sb.tile([P, NQ], U32, name="q_codes", align_bytes=64)
         q_sc = sb.tile([P, NQ], U8, name="q_sc", align_bytes=64)
@@ -144,6 +151,10 @@ def tile_attend_pkv8_soft_sink_kb_kernel(
         turned = {}
 
         def scores(g):
+            if g == LAST:
+                ks_last = reuse.tile([P, PAGE], U8, name="ks_last", offset=KW0_AT, align_bytes=64)
+                nc.vector.tensor_copy(ks_last[:], ks_pool[:].indirect(page_offs(g)))
+                ks.append(ks_last[:])
             nc.vector.tensor_copy(kw[g][:], kw_pool[:].bitcast(U32).indirect(page_offs(g)))
             for pair in range(PACK // 2):
                 bank = bank_tile([P, 2, NQ], "score", score_banks[g][pair])
@@ -152,7 +163,7 @@ def tile_attend_pkv8_soft_sink_kb_kernel(
                     nc.tensor.matmul_mx(
                         out=bank[:, jj, :],
                         lhsT=kw[g][:, j * P : (j + 1) * P].bitcast(FP8X4),
-                        lhsT_scale=ks[:, g * PAGE + j * P : g * PAGE + (j + 1) * P],
+                        lhsT_scale=ks[g][:, j * P : (j + 1) * P],
                         rhs=q_codes[:].bitcast(FP8X4),
                         rhs_scale=q_sc[:],
                         start=True,
@@ -178,11 +189,9 @@ def tile_attend_pkv8_soft_sink_kb_kernel(
             turn(g - 1)
         turn(LAST)
 
-        vs_page = [
-            reuse.tile([P, PAGE], F32, name="vs_page0", offset=KB_COL_AT, align_bytes=64)[:],
-            reuse.tile([P, PAGE], F32, name="vs_page1", offset=KW0_AT, align_bytes=64)[:],
-        ]
-        nc.vector.tensor_copy(vs_page[1], vs_pool[:].indirect(page_offs(1)))
+        vs_page[LAST] = reuse.tile([P, PAGE], F32, name="vs_page2", offset=KW1_AT, align_bytes=64)[:]
+        nc.vector.tensor_copy(vs_page[LAST], vs_pool[:].indirect(page_offs(LAST)))
+        vs_page[0] = reuse.tile([P, PAGE], F32, name="vs_page0", offset=KB_COL_AT, align_bytes=64)[:]
         nc.scalar.activation(vs_page[0], vs_pool[:].indirect(page_offs(0)), ACT.Copy)
 
         neg_s = {}
@@ -207,9 +216,7 @@ def tile_attend_pkv8_soft_sink_kb_kernel(
                     accum_out=mins[g, c][:, 0:1],
                 )
 
-        vs_page.append(reuse.tile([P, PAGE], F32, name="vs_page2", offset=MIN_AT, align_bytes=64)[:])
-        nc.vector.tensor_copy(vs_page[LAST], vs_pool[:].indirect(page_offs(LAST)))
-        vw_at = MIN_AT + PAGE * WORD
+        vw_at = MIN_AT
         vw = reuse.tile([P, PAGES * DV], U32, name="vw", offset=vw_at, align_bytes=64)
         vsc = reuse.tile([P, PAGES * DV], U8, name="vsc", offset=vw_at + PAGES * DV * WORD, align_bytes=64)
         nc.vector.tensor_copy(vw[:], vw_pool[:].bitcast(U32).indirect(voffs_t[:]))
@@ -217,7 +224,6 @@ def tile_attend_pkv8_soft_sink_kb_kernel(
 
         sums = sb.tile([P, HALVES, PAGES], F32, name="sums")
         p_banks = {}
-        wide = [bank_tile([P, 2, NQ], "p_wide", pair) for pair in range(PACK // 2)]
         for c in range(HALVES):
             for g in range(PAGES):
                 prob = sb.tile([P, PAGE + 1 if g == LAST else PAGE], F32, name=f"prob{g}{c}")
@@ -225,20 +231,17 @@ def tile_attend_pkv8_soft_sink_kb_kernel(
                     prob[:], neg_s[g, c], ACT.Exp, bias=mins[LAST, c][:], scale=-1.0,
                     accum_out=sums[:, c, g : g + 1],
                 )
-                if g > 0:
-                    p_banks[g, c] = bank_tile([P, PACK, P], "p_turned", 4 + LAST * c + g - 1)
+                p_banks[g, c] = bank_tile([P, PACK, P], "p_turned", P_BANKS[PAGES * c + g])
                 for t in range(PACK):
-                    dst = wide[t // 2][:, t % 2, c * P : (c + 1) * P] if g == 0 else p_banks[g, c][:, t, :]
-                    nc.tensor.transpose(dst, prob[:, t * P : (t + 1) * P], ident[:])
+                    nc.tensor.transpose(p_banks[g, c][:, t, :], prob[:, t * P : (t + 1) * P], ident[:])
         y_banks = [bank_tile([P, DV], f"y{c}", 2 + c) for c in range(HALVES)]
 
         w = {}
-        places = sb.tile([P, PACK, NQ], BF16, name="places")
+        places = sb.tile([P, PACK, P], BF16, name="places")
         for t in range(PACK):
-            nc.scalar.activation(places[:, t, :], wide[t // 2][:, t % 2, :], ACT.Copy, scale=vs_page[0][:, t : t + 1])
-        for c in range(HALVES):
-            w[0, c] = sb.tile([P, P, PACK], BF16, name=f"w0{c}", align_bytes=64)
-            nc.scalar.copy(w[0, c][:], places[:, :, c * P : (c + 1) * P].rearrange("p t m -> p m t"))
+            nc.scalar.activation(places[:, t, :], p_banks[0, 1][:, t, :], ACT.Copy, scale=vs_page[0][:, t : t + 1])
+        w[0, 1] = sb.tile([P, P, PACK], BF16, name="w01", align_bytes=64)
+        nc.scalar.copy(w[0, 1][:], places[:].rearrange("p t m -> p m t"))
 
         def weigh_on_vector(g, c):
             w[g, c] = sb.tile([P, P, PACK], BF16, name=f"w{g}{c}", align_bytes=64)
@@ -270,14 +273,15 @@ def tile_attend_pkv8_soft_sink_kb_kernel(
 
         total = sb.tile([P, HALVES], F32, name="total")
         inv = sb.tile([P, HALVES], F32, name="inv")
+        weigh_on_vector(0, 0)
         weigh_on_vector(1, 0)
-        nc.vector.tensor_reduce(total[:], sums[:], AX.X, ALU.add)
+        multiply(0, 0)
         weigh_on_vector(2, 0)
-        nc.vector.reciprocal(inv[:], total[:])
         multiply(1, 0)
+        nc.vector.tensor_reduce(total[:], sums[:], AX.X, ALU.add)
         weigh_on_vector(1, 1)
         multiply(2, 0)
-        multiply(0, 0)
+        nc.vector.reciprocal(inv[:], total[:])
         weigh_on_vector(2, 1)
         multiply(1, 1)
         multiply(0, 1)

@@ -81,15 +81,15 @@ def tile_attend_pkv8_soft_sink_kb_kernel(
         nc.sync.dma_start(q_raw[:], qT[0].rearrange("(p j) q -> p j q", j=PACK))
         for a in range(QUADRANTS):
             nc.scalar.dma_start(
-                ks_pool[32 * a : 32 * a + 4, :].bitcast(I32), k_scales[0, 4 * a : 4 * a + 4, :].bitcast(I32)
+                ks_pool[a:P:32, :].bitcast(I32), k_scales[0, a:16:4, :].bitcast(I32)
             )
         nc.sync.dma_start(kw_pool[:], k_words[0].rearrange("p t r -> p (t r)").bitcast(I32))
         nc.sync.dma_start(sink_t[:], sink[0].rearrange("(p c) o -> p (c o)", c=HALVES))
         nc.sync.dma_start(voffs_t[:], voffs)
         for a in range(QUADRANTS):
             nc.sync.dma_start(
-                vsc_pool[32 * a : 32 * a + 4, :].bitcast(I32).rearrange("f (u e) -> f u e", e=DV // WORD),
-                v_scales[:, 4 * a : 4 * a + 4, :].rearrange("u f e -> f u e").bitcast(I32),
+                vsc_pool[a:P:32, :].bitcast(I32).rearrange("f (u e) -> f u e", e=DV // WORD),
+                v_scales[:, a:16:4, :].rearrange("u f e -> f u e").bitcast(I32),
             )
 
         q_bf = sb.tile([P, HALVES, P, PACK], BF16, name="q_bf", align_bytes=64)
@@ -105,25 +105,28 @@ def tile_attend_pkv8_soft_sink_kb_kernel(
         vs_bank = bank_tile([P, PACK, P], "vs_bank", 7)
         for t in range(PACK):
             nc.tensor.transpose(vs_bank[:, t, :], vs_in[:, t:PAGE:PACK], ident[:])
-        vs_small = reuse.tile([P, POOL_PAGES, PACK], F32, name="vs_small", offset=VS_SMALL_AT, align_bytes=64)
-        nc.vector.tensor_copy(vs_small[:], vs_bank[:, :, VS_ROW0:P].rearrange("p t u -> p u t"))
+        small_tile = reuse.tile([P, 2 * PAGE], F32, name="small_tile", offset=VS_SMALL_AT, align_bytes=64)
+        vs_small = small_tile[:, 0 : POOL_PAGES * PACK].rearrange("p (u t) -> p u t", t=PACK)
+        nc.vector.tensor_copy(vs_small, vs_bank[:, :, VS_ROW0:P].rearrange("p t u -> p u t"))
 
         vs_pool = sb.tile([P, T], F32, name="vs_pool")
         nc.vector.tensor_copy(
             vs_pool[:].rearrange("p (u r t) -> p u r t", u=POOL_PAGES, t=PACK),
-            vs_small[:].unsqueeze(2).to_broadcast([P, POOL_PAGES, P, PACK]),
+            vs_small.unsqueeze(2).to_broadcast([P, POOL_PAGES, P, PACK]),
         )
-
-        vs_page = {1: sb.tile([P, PAGE], F32, name="vs_page1")[:]}
-        nc.vector.tensor_copy(vs_page[1], vs_pool[:].indirect(page_offs(1)))
 
         kb_bank = bank_tile([P, P + 2 * PAGES * PACK], "kb_bank", 6)
         for g in range(PAGES):
-            kb_row = sb.tile([P, PAGE], F32, name=f"kb_row{g}")
+            if g == LAST:
+                kb_row = reuse.tile([P, PAGE], F32, name="kb_last", offset=VS_SMALL_AT + PAGE * WORD, align_bytes=64)
+            else:
+                kb_row = sb.tile([P, PAGE], F32, name=f"kb_row{g}")
             nc.scalar.activation(kb_row[:], kb_pool[:].indirect(page_offs(g)), ACT.Copy)
             for j in reversed(range(PACK)):
                 at = 2 * ((LAST - g) * PACK + j)
                 nc.tensor.transpose(kb_bank[:, at : at + P], kb_row[:, j * P : (j + 1) * P], ident[:])
+        vs_page = {1: sb.tile([P, PAGE], F32, name="vs_page1")[:]}
+        nc.scalar.activation(vs_page[1], vs_pool[:].indirect(page_offs(1)), ACT.Copy)
         kb_col = reuse.tile([P, PAGES * PACK], F32, name="kb_col", offset=KB_COL_AT, align_bytes=64)
         nc.scalar.copy(kb_col[:], kb_bank[:, LIVE : LIVE + 2 * PAGES * PACK : 2])
 
@@ -132,9 +135,8 @@ def tile_attend_pkv8_soft_sink_kb_kernel(
             reuse.tile([P, PAGE], U32, name="kw1", offset=KW1_AT, align_bytes=64),
             sb.tile([P, PAGE], U32, name="kw2", align_bytes=64),
         ]
-        ks_early = reuse.tile([P, LAST * PAGE], U8, name="ks_early", offset=VS_SMALL_AT, align_bytes=64)
-        nc.vector.tensor_copy(ks_early[:], ks_pool[:].indirect(offs_t[:, 0 : LAST * LIST_COLS]))
-        ks = [ks_early[:, g * PAGE : (g + 1) * PAGE] for g in range(LAST)]
+        ks = reuse.tile([P, N], U8, name="ks", offset=VS_SMALL_AT, align_bytes=64)
+        nc.vector.tensor_copy(ks[:], ks_pool[:].indirect(offs_t[:]))
 
         q_codes = sb.tile([P, NQ], U32, name="q_codes", align_bytes=64)
         q_sc = sb.tile([P, NQ], U8, name="q_sc", align_bytes=64)
@@ -151,10 +153,6 @@ def tile_attend_pkv8_soft_sink_kb_kernel(
         turned = {}
 
         def scores(g):
-            if g == LAST:
-                ks_last = reuse.tile([P, PAGE], U8, name="ks_last", offset=KW0_AT, align_bytes=64)
-                nc.vector.tensor_copy(ks_last[:], ks_pool[:].indirect(page_offs(g)))
-                ks.append(ks_last[:])
             nc.vector.tensor_copy(kw[g][:], kw_pool[:].bitcast(U32).indirect(page_offs(g)))
             for pair in range(PACK // 2):
                 bank = bank_tile([P, 2, NQ], "score", score_banks[g][pair])
@@ -163,7 +161,7 @@ def tile_attend_pkv8_soft_sink_kb_kernel(
                     nc.tensor.matmul_mx(
                         out=bank[:, jj, :],
                         lhsT=kw[g][:, j * P : (j + 1) * P].bitcast(FP8X4),
-                        lhsT_scale=ks[g][:, j * P : (j + 1) * P],
+                        lhsT_scale=ks[:, g * PAGE + j * P : g * PAGE + (j + 1) * P],
                         rhs=q_codes[:].bitcast(FP8X4),
                         rhs_scale=q_sc[:],
                         start=True,

@@ -153,7 +153,12 @@ def tile_attend_pkv8_soft_sink_kb_kernel(
         turned = {}
 
         def scores(g):
-            nc.vector.tensor_copy(kw[g][:], kw_pool[:].bitcast(U32).indirect(page_offs(g)))
+            pieces = 2 if g == 0 else 1
+            for piece in range(pieces):
+                first, end = piece * PAGE // pieces, (piece + 1) * PAGE // pieces
+                nc.vector.tensor_copy(
+                    kw[g][:, first:end], kw_pool[:].bitcast(U32).indirect(page_offs(g)[:, first // 16 : end // 16])
+                )
             for pair in range(PACK // 2):
                 bank = bank_tile([P, 2, NQ], "score", score_banks[g][pair])
                 for jj in range(2):

@@ -30,8 +30,8 @@ WORD = 4
 
 Q_RAW_AT = 0
 KW0_AT = 4096
-KW1_AT = 6144
 KB_COL_AT = 8192
+VS_IN_AT = 12288
 MIN_AT = 16384
 VS_SMALL_AT = 32768
 MIN_COLS = PAGES * DV + PAGES * DV // WORD
@@ -61,9 +61,9 @@ def tile_attend_pkv8_soft_sink_kb_kernel(
         voffs_t = sb.tile([P, PAGES * DV // 16], U16, name="voffs_t")
         kw_pool = sb.tile([P, T], I32, name="kw_pool")
         ks_pool = sb.tile([P, T], U8, name="ks_pool")
-        vsc_pool = sb.tile([P, T // PAGE * DV], U8, name="vsc_pool")
+        vsc_pool = reuse.tile([P, T // PAGE * DV], U8, name="vsc_pool", offset=VS_IN_AT, align_bytes=64)
         kb_pool = sb.tile([P, T], F32, name="kb_pool")
-        vs_in = sb.tile([P, PAGE], F32, name="vs_in")
+        vs_in = reuse.tile([P, PAGE], F32, name="vs_in", offset=VS_IN_AT, align_bytes=64)
         sink_t = sb.tile([P, HALVES], F32, name="sink_t")
         ident = sb.tile([P, P], F32, name="ident")
         q_raw = reuse.tile([P, PACK, NQ], F32, name="q_raw", offset=Q_RAW_AT, align_bytes=64)
@@ -72,7 +72,6 @@ def tile_attend_pkv8_soft_sink_kb_kernel(
         nc.vector.memset(ks_pool[:].bitcast(I32), 0)
         nc.vector.memset(vs_in[0:VS_ROW0, :], 0.0)
         nc.vector.memset(kb_pool[0:LIVE, :], 0.0)
-        nc.vector.memset(vsc_pool[:].bitcast(I32), 0)
         make_identity(nc, ident[:])
 
         nc.sync.dma_start(offs_t[:], offs)
@@ -86,16 +85,11 @@ def tile_attend_pkv8_soft_sink_kb_kernel(
         nc.sync.dma_start(kw_pool[:], k_words[0].rearrange("p t r -> p (t r)").bitcast(I32))
         nc.sync.dma_start(sink_t[:], sink[0].rearrange("(p c) o -> p (c o)", c=HALVES))
         nc.sync.dma_start(voffs_t[:], voffs)
-        for a in range(QUADRANTS):
-            nc.sync.dma_start(
-                vsc_pool[a:P:32, :].bitcast(I32).rearrange("f (u e) -> f u e", e=DV // WORD),
-                v_scales[:, a:16:4, :].rearrange("u f e -> f u e").bitcast(I32),
-            )
 
         q_bf = sb.tile([P, HALVES, P, PACK], BF16, name="q_bf", align_bytes=64)
         q_view = q_raw[:].rearrange("p j (m c) -> p c m j", c=HALVES)
-        for c in range(HALVES):
-            nc.scalar.activation(q_bf[:, c], q_view[:, c], ACT.Copy)
+        nc.scalar.activation(q_bf[:, 0], q_view[:, 0], ACT.Copy)
+        nc.vector.tensor_copy(q_bf[:, 1], q_view[:, 1])
 
         nc.sync.dma_start(
             vw_pool[:].rearrange("p (u e) -> p u e", e=DV),
@@ -108,6 +102,13 @@ def tile_attend_pkv8_soft_sink_kb_kernel(
         small_tile = reuse.tile([P, 2 * PAGE], F32, name="small_tile", offset=VS_SMALL_AT, align_bytes=64)
         vs_small = small_tile[:, 0 : POOL_PAGES * PACK].rearrange("p (u t) -> p u t", t=PACK)
         nc.vector.tensor_copy(vs_small, vs_bank[:, :, VS_ROW0:P].rearrange("p t u -> p u t"))
+
+        nc.vector.memset(vsc_pool[:].bitcast(I32), 0)
+        for a in range(QUADRANTS):
+            nc.sync.dma_start(
+                vsc_pool[a:P:32, :].bitcast(I32).rearrange("f (u e) -> f u e", e=DV // WORD),
+                v_scales[:, a:16:4, :].rearrange("u f e -> f u e").bitcast(I32),
+            )
 
         vs_pool = sb.tile([P, T], F32, name="vs_pool")
         nc.vector.tensor_copy(
@@ -132,7 +133,7 @@ def tile_attend_pkv8_soft_sink_kb_kernel(
 
         kw = [
             reuse.tile([P, PAGE], U32, name="kw0", offset=KW0_AT, align_bytes=64),
-            reuse.tile([P, PAGE], U32, name="kw1", offset=KW1_AT, align_bytes=64),
+            sb.tile([P, PAGE], U32, name="kw1", align_bytes=64),
             sb.tile([P, PAGE], U32, name="kw2", align_bytes=64),
         ]
         ks = reuse.tile([P, N], U8, name="ks", offset=VS_SMALL_AT, align_bytes=64)
@@ -192,7 +193,7 @@ def tile_attend_pkv8_soft_sink_kb_kernel(
             turn(g - 1)
         turn(LAST)
 
-        vs_page[LAST] = reuse.tile([P, PAGE], F32, name="vs_page2", offset=KW1_AT, align_bytes=64)[:]
+        vs_page[LAST] = reuse.tile([P, PAGE], F32, name="vs_page2", offset=KW0_AT, align_bytes=64)[:]
         nc.vector.tensor_copy(vs_page[LAST], vs_pool[:].indirect(page_offs(LAST)))
         vs_page[0] = reuse.tile([P, PAGE], F32, name="vs_page0", offset=KB_COL_AT, align_bytes=64)[:]
         nc.scalar.activation(vs_page[0], vs_pool[:].indirect(page_offs(0)), ACT.Copy)

@@ -37,6 +37,7 @@ VS_SMALL_AT = 32768
 MIN_COLS = PAGES * DV + PAGES * DV // WORD
 
 P_BANKS = (0, 1, 4, 5, 6, 7)
+Y_BANKS = (6, 5)
 
 FLOPS = 2 * NQ * N * (D + DV)
 BYTES = D * NQ * 4 + T * (D + DV) + T * (D + DV) // 32 + 2 * T * 4 + NQ * 4 + P * (N + PAGES * DV) // 8 + NQ * DV * 4
@@ -238,7 +239,6 @@ def tile_attend_pkv8_soft_sink_kb_kernel(
                 p_banks[g, c] = bank_tile([P, PACK, P], "p_turned", P_BANKS[PAGES * c + g])
                 for t in range(PACK):
                     nc.tensor.transpose(p_banks[g, c][:, t, :], prob[:, t * P : (t + 1) * P], ident[:])
-        y_banks = [bank_tile([P, DV], f"y{c}", 2 + c) for c in range(HALVES)]
 
         w = {}
         places = sb.tile([P, PACK, P], BF16, name="places")
@@ -256,40 +256,45 @@ def tile_attend_pkv8_soft_sink_kb_kernel(
                 ALU.mult,
             )
 
-        passes = []
+        quantised = {}
 
-        def multiply(g, c):
+        def quantise(g, c):
             codes = sb.tile([P, P], U32, name=f"w_codes{g}{c}", align_bytes=64)
             scales = sb.tile([P, P], U8, name=f"w_sc{g}{c}", align_bytes=64)
             nc.vector.quantize_mx(
                 out=codes[:].bitcast(FP8X4), scales=scales[:], in_=w[g, c][:].rearrange("p m t -> p (m t)")
             )
-            passes.append(c)
-            nc.tensor.matmul_mx(
-                out=y_banks[c][:],
-                lhsT=codes[:].bitcast(FP8X4),
-                lhsT_scale=scales[:],
-                rhs=vw[:, g * DV : (g + 1) * DV].bitcast(FP8X4),
-                rhs_scale=vsc[:, g * DV : (g + 1) * DV],
-                start=(passes.count(c) == 1),
-                stop=(passes.count(c) == PAGES),
-            )
+            quantised[g, c] = (codes, scales)
 
         total = sb.tile([P, HALVES], F32, name="total")
         inv = sb.tile([P, HALVES], F32, name="inv")
         weigh_on_vector(0, 0)
         weigh_on_vector(1, 0)
-        multiply(0, 0)
+        quantise(0, 0)
         weigh_on_vector(2, 0)
-        multiply(1, 0)
+        quantise(1, 0)
         nc.vector.tensor_reduce(total[:], sums[:], AX.X, ALU.add)
         weigh_on_vector(1, 1)
-        multiply(2, 0)
+        quantise(2, 0)
         nc.vector.reciprocal(inv[:], total[:])
         weigh_on_vector(2, 1)
-        multiply(1, 1)
-        multiply(0, 1)
-        multiply(2, 1)
+        quantise(1, 1)
+        quantise(0, 1)
+        quantise(2, 1)
+        y_banks = []
+        for c, pages in enumerate(((0, 1, 2), (1, 0, 2))):
+            y_banks.append(bank_tile([P, DV], f"y{c}", Y_BANKS[c]))
+            for g in pages:
+                codes, scales = quantised[g, c]
+                nc.tensor.matmul_mx(
+                    out=y_banks[c][:],
+                    lhsT=codes[:].bitcast(FP8X4),
+                    lhsT_scale=scales[:],
+                    rhs=vw[:, g * DV : (g + 1) * DV].bitcast(FP8X4),
+                    rhs_scale=vsc[:, g * DV : (g + 1) * DV],
+                    start=(g == pages[0]),
+                    stop=(g == pages[-1]),
+                )
 
         y_sb = sb.tile([P, HALVES, DV], F32, name="y_sb")
         out_view = out[0].rearrange("(p c) e -> p c e", c=HALVES)

from contextlib import ExitStack

import concourse.mybir as mybir
from concourse.masks import make_identity

F32 = mybir.dt.float32
BF16 = mybir.dt.bfloat16
I32 = mybir.dt.int32
U32 = mybir.dt.uint32
U16 = mybir.dt.uint16
U8 = mybir.dt.uint8
FP8X4 = mybir.dt.float8_e4m3fn_x4
ALU = mybir.AluOpType
ACT = mybir.ActivationFunctionType
AX = mybir.AxisListType

P = 128
PACK = 4
NQ, N, T, D, DV = 256, 1536, 4096, 512, 128
PAGE = 512
PAGES = N // PAGE
HALVES = NQ // P
LAST = PAGES - 1
POOL_PAGES = T // PAGE
LIVE = P - 1
VS_ROW0 = P - POOL_PAGES
QUADRANTS = 4
LIST_COLS = PAGE // 16
WORD = 4

Q_RAW_AT = 0
KW0_AT = 4096
KB_COL_AT = 8192
VS_IN_AT = 12288
MIN_AT = 16384
VS_SMALL_AT = 32768
MIN_COLS = PAGES * DV + PAGES * DV // WORD

P_BANKS = (0, 1, 4, 5, 6, 7)
Y_BANKS = (6, 5)

FLOPS = 2 * NQ * N * (D + DV)
BYTES = D * NQ * 4 + T * (D + DV) + T * (D + DV) // 32 + 2 * T * 4 + NQ * 4 + P * (N + PAGES * DV) // 8 + NQ * DV * 4


def tile_attend_pkv8_soft_sink_kb_kernel(
    tc, qT, k_words, k_scales, v_words, v_scales, vs, kb, sink, offs, voffs, out
):
    nc = tc.nc
    with ExitStack() as ctx:
        sb = ctx.enter_context(tc.tile_pool(name="sb", bufs=1))
        reuse = ctx.enter_context(tc.tile_pool(name="reuse", bufs=1))
        ps = ctx.enter_context(tc.psum_pool(name="ps", bufs=1))

        def bank_tile(shape, name, bank):
            return ps.tile(shape, F32, name=name, tag=f"bank{bank}")

        def page_offs(g):
            return offs_t[:, g * LIST_COLS : (g + 1) * LIST_COLS]

        offs_t = sb.tile([P, N // 16], U16, name="offs_t")
        voffs_t = sb.tile([P, PAGES * DV // 16], U16, name="voffs_t")
        kw_pool = sb.tile([P, T], I32, name="kw_pool")
        ks_pool = sb.tile([P, T], U8, name="ks_pool")
        vsc_pool = reuse.tile([P, T // PAGE * DV], U8, name="vsc_pool", offset=VS_IN_AT, align_bytes=64)
        kb_pool = sb.tile([P, T], F32, name="kb_pool")
        vs_in = reuse.tile([P, PAGE], F32, name="vs_in", offset=VS_IN_AT, align_bytes=64)
        sink_t = sb.tile([P, HALVES], F32, name="sink_t")
        ident = sb.tile([P, P], F32, name="ident")
        q_raw = reuse.tile([P, PACK, NQ], F32, name="q_raw", offset=Q_RAW_AT, align_bytes=64)
        vw_pool = reuse.tile([P, T // PAGE * DV], I32, name="vw_pool", offset=Q_RAW_AT, align_bytes=64)

        nc.vector.memset(ks_pool[:].bitcast(I32), 0)
        nc.vector.memset(vs_in[0:VS_ROW0, :], 0.0)
        nc.vector.memset(kb_pool[0:LIVE, :], 0.0)
        make_identity(nc, ident[:])

        nc.sync.dma_start(offs_t[:], offs)
        nc.sync.dma_start(vs_in[VS_ROW0:P, :], vs[0].rearrange("(u j) -> u j", j=PAGE))
        nc.sync.dma_start(kb_pool[LIVE:P, :], kb[0:1, :])
        nc.sync.dma_start(q_raw[:], qT[0].rearrange("(p j) q -> p j q", j=PACK))
        for a in range(QUADRANTS):
            nc.scalar.dma_start(
                ks_pool[a:P:32, :].bitcast(I32), k_scales[0, a:16:4, :].bitcast(I32)
            )
        nc.sync.dma_start(kw_pool[:], k_words[0].rearrange("p t r -> p (t r)").bitcast(I32))
        nc.sync.dma_start(sink_t[:], sink[0].rearrange("(p c) o -> p (c o)", c=HALVES))
        nc.sync.dma_start(voffs_t[:], voffs)

        q_bf = sb.tile([P, HALVES, P, PACK], BF16, name="q_bf", align_bytes=64)
        q_view = q_raw[:].rearrange("p j (m c) -> p c m j", c=HALVES)
        nc.scalar.activation(q_bf[:, 0], q_view[:, 0], ACT.Copy)
        nc.vector.tensor_copy(q_bf[:, 1], q_view[:, 1])

        nc.sync.dma_start(
            vw_pool[:].rearrange("p (u e) -> p u e", e=DV),
            v_words.rearrange("u p e r -> p u (e r)").bitcast(I32),
        )

        vs_bank = bank_tile([P, PACK, P], "vs_bank", 7)
        for t in range(PACK):
            nc.tensor.transpose(vs_bank[:, t, :], vs_in[:, t:PAGE:PACK], ident[:])
        small_tile = reuse.tile([P, 2 * PAGE], F32, name="small_tile", offset=VS_SMALL_AT, align_bytes=64)
        vs_small = small_tile[:, 0 : POOL_PAGES * PACK].rearrange("p (u t) -> p u t", t=PACK)
        nc.vector.tensor_copy(vs_small, vs_bank[:, :, VS_ROW0:P].rearrange("p t u -> p u t"))

        nc.vector.memset(vsc_pool[:].bitcast(I32), 0)
        for a in range(QUADRANTS):
            nc.sync.dma_start(
                vsc_pool[a:P:32, :].bitcast(I32).rearrange("f (u e) -> f u e", e=DV // WORD),
                v_scales[:, a:16:4, :].rearrange("u f e -> f u e").bitcast(I32),
            )

        vs_pool = sb.tile([P, T], F32, name="vs_pool")
        nc.vector.tensor_copy(
            vs_pool[:].rearrange("p (u r t) -> p u r t", u=POOL_PAGES, t=PACK),
            vs_small.unsqueeze(2).to_broadcast([P, POOL_PAGES, P, PACK]),
        )

        kb_bank = bank_tile([P, P + 2 * PAGES * PACK], "kb_bank", 6)
        for g in range(PAGES):
            if g == LAST:
                kb_row = reuse.tile([P, PAGE], F32, name="kb_last", offset=VS_SMALL_AT + PAGE * WORD, align_bytes=64)
            else:
                kb_row = sb.tile([P, PAGE], F32, name=f"kb_row{g}")
            nc.scalar.activation(kb_row[:], kb_pool[:].indirect(page_offs(g)), ACT.Copy)
            for j in reversed(range(PACK)):
                at = 2 * ((LAST - g) * PACK + j)
                nc.tensor.transpose(kb_bank[:, at : at + P], kb_row[:, j * P : (j + 1) * P], ident[:])
        vs_page = {1: sb.tile([P, PAGE], F32, name="vs_page1")[:]}
        nc.scalar.activation(vs_page[1], vs_pool[:].indirect(page_offs(1)), ACT.Copy)
        kb_col = reuse.tile([P, PAGES * PACK], F32, name="kb_col", offset=KB_COL_AT, align_bytes=64)
        nc.scalar.copy(kb_col[:], kb_bank[:, LIVE : LIVE + 2 * PAGES * PACK : 2])

        kw = [
            reuse.tile([P, PAGE], U32, name="kw0", offset=KW0_AT, align_bytes=64),
            sb.tile([P, PAGE], U32, name="kw1", align_bytes=64),
            sb.tile([P, PAGE], U32, name="kw2", align_bytes=64),
        ]
        ks = reuse.tile([P, N], U8, name="ks", offset=VS_SMALL_AT, align_bytes=64)
        nc.vector.tensor_copy(ks[:], ks_pool[:].indirect(offs_t[:]))

        q_codes = sb.tile([P, NQ], U32, name="q_codes", align_bytes=64)
        q_sc = sb.tile([P, NQ], U8, name="q_sc", align_bytes=64)
        nc.vector.quantize_mx(
            out=q_codes[:].bitcast(FP8X4), scales=q_sc[:], in_=q_bf[:].rearrange("p c m j -> p (c m j)")
        )

        neg_s_last = sb.tile([P, HALVES, PAGE + 8], F32, name="neg_s_last")
        nc.gpsimd.tensor_scalar(neg_s_last[:, :, PAGE], sink_t[:], -1.0, 0.0, ALU.mult, ALU.add)

        s_turned = [sb.tile([P, PACK, NQ], F32, name=f"s_turned{g}") for g in range(PAGES)]
        score_banks = ((0, 1), (2, 3), (0, 1))
        turn_banks = ((4, 5), (6, 7), (2, 3))
        turned = {}

        def scores(g):
            pieces = 2 if g == 0 else 1
            for piece in range(pieces):
                first, end = piece * PAGE // pieces, (piece + 1) * PAGE // pieces
                nc.vector.tensor_copy(
                    kw[g][:, first:end], kw_pool[:].bitcast(U32).indirect(page_offs(g)[:, first // 16 : end // 16])
                )
            for pair in range(PACK // 2):
                bank = bank_tile([P, 2, NQ], "score", score_banks[g][pair])
                for jj in range(2):
                    j = 2 * pair + jj
                    nc.tensor.matmul_mx(
                        out=bank[:, jj, :],
                        lhsT=kw[g][:, j * P : (j + 1) * P].bitcast(FP8X4),
                        lhsT_scale=ks[:, g * PAGE + j * P : g * PAGE + (j + 1) * P],
                        rhs=q_codes[:].bitcast(FP8X4),
                        rhs_scale=q_sc[:],
                        start=True,
                        stop=True,
                    )
                for jj in range(2):
                    j = 2 * pair + jj
                    nc.scalar.activation(
                        s_turned[g][:, j, :], bank[:, jj, :], ACT.Identity, bias=kb_col[:, (LAST - g) * PACK + j : (LAST - g) * PACK + j + 1]
                    )

        def turn(g):
            for c in range(HALVES):
                turned[g, c] = bank_tile([P, PAGE], "turned", turn_banks[g][c])
                for j in range(PACK):
                    nc.tensor.transpose(
                        turned[g, c][:, j * P : (j + 1) * P], s_turned[g][:, j, c * P : (c + 1) * P], ident[:]
                    )

        scores(0)
        for g in range(1, PAGES):
            scores(g)
            turn(g - 1)
        turn(LAST)

        vs_page[LAST] = reuse.tile([P, PAGE], F32, name="vs_page2", offset=KW0_AT, align_bytes=64)[:]
        nc.vector.tensor_copy(vs_page[LAST], vs_pool[:].indirect(page_offs(LAST)))
        vs_page[0] = reuse.tile([P, PAGE], F32, name="vs_page0", offset=KB_COL_AT, align_bytes=64)[:]
        nc.scalar.activation(vs_page[0], vs_pool[:].indirect(page_offs(0)), ACT.Copy)

        neg_s = {}
        mins = {}
        for g in range(PAGES):
            for c in range(HALVES):
                if g == LAST:
                    neg_s[g, c] = neg_s_last[:, c, 0 : PAGE + 1]
                else:
                    neg_s[g, c] = sb.tile([P, PAGE], F32, name=f"neg_s{g}{c}")[:]
                if (g, c) == (LAST - 1, 0):
                    mins[g, c] = reuse.tile([P, MIN_COLS], F32, name="min_mid", offset=MIN_AT, align_bytes=64)
                else:
                    mins[g, c] = sb.tile([P, 1], F32, name=f"min{g}{c}")
                nc.vector.tensor_scalar(
                    neg_s[g, c][:, 0:PAGE].rearrange("q (t z) -> q t z", t=PACK),
                    turned[g, c][:].rearrange("q (z t) -> q t z", t=PACK),
                    -1.0,
                    neg_s_last[:, c, PAGE : PAGE + 1] if g == 0 else mins[g - 1, c][:, 0:1],
                    ALU.mult,
                    ALU.min,
                    accum_out=mins[g, c][:, 0:1],
                )

        vw_at = MIN_AT
        vw = reuse.tile([P, PAGES * DV], U32, name="vw", offset=vw_at, align_bytes=64)
        vsc = reuse.tile([P, PAGES * DV], U8, name="vsc", offset=vw_at + PAGES * DV * WORD, align_bytes=64)
        nc.vector.tensor_copy(vw[:], vw_pool[:].bitcast(U32).indirect(voffs_t[:]))
        nc.vector.tensor_copy(vsc[:], vsc_pool[:].indirect(voffs_t[:]))

        sums = sb.tile([P, HALVES, PAGES], F32, name="sums")
        p_banks = {}
        for c in range(HALVES):
            for g in range(PAGES):
                prob = sb.tile([P, PAGE + 1 if g == LAST else PAGE], F32, name=f"prob{g}{c}")
                nc.scalar.activation(
                    prob[:], neg_s[g, c], ACT.Exp, bias=mins[LAST, c][:], scale=-1.0,
                    accum_out=sums[:, c, g : g + 1],
                )
                p_banks[g, c] = bank_tile([P, PACK, P], "p_turned", P_BANKS[PAGES * c + g])
                for t in range(PACK):
                    nc.tensor.transpose(p_banks[g, c][:, t, :], prob[:, t * P : (t + 1) * P], ident[:])

        w = {}
        places = sb.tile([P, PACK, P], BF16, name="places")
        for t in range(PACK):
            nc.scalar.activation(places[:, t, :], p_banks[0, 1][:, t, :], ACT.Copy, scale=vs_page[0][:, t : t + 1])
        w[0, 1] = sb.tile([P, P, PACK], BF16, name="w01", align_bytes=64)
        nc.scalar.copy(w[0, 1][:], places[:].rearrange("p t m -> p m t"))

        def weigh_on_vector(g, c):
            w[g, c] = sb.tile([P, P, PACK], BF16, name=f"w{g}{c}", align_bytes=64)
            nc.vector.tensor_tensor(
                w[g, c][:],
                p_banks[g, c][:].rearrange("p t m -> p m t"),
                vs_page[g].rearrange("p (m t) -> p m t", t=PACK),
                ALU.mult,
            )

        quantised = {}

        def quantise(g, c):
            codes = sb.tile([P, P], U32, name=f"w_codes{g}{c}", align_bytes=64)
            scales = sb.tile([P, P], U8, name=f"w_sc{g}{c}", align_bytes=64)
            nc.vector.quantize_mx(
                out=codes[:].bitcast(FP8X4), scales=scales[:], in_=w[g, c][:].rearrange("p m t -> p (m t)")
            )
            quantised[g, c] = (codes, scales)

        total = sb.tile([P, HALVES], F32, name="total")
        inv = sb.tile([P, HALVES], F32, name="inv")
        weigh_on_vector(0, 0)
        weigh_on_vector(1, 0)
        quantise(0, 0)
        weigh_on_vector(2, 0)
        quantise(1, 0)
        nc.vector.tensor_reduce(total[:], sums[:], AX.X, ALU.add)
        weigh_on_vector(1, 1)
        quantise(2, 0)
        nc.vector.reciprocal(inv[:], total[:])
        weigh_on_vector(2, 1)
        quantise(1, 1)
        quantise(0, 1)
        quantise(2, 1)
        y_banks = []
        for c, pages in enumerate(((0, 1, 2), (1, 0, 2))):
            y_banks.append(bank_tile([P, DV], f"y{c}", Y_BANKS[c]))
            for g in pages:
                codes, scales = quantised[g, c]
                nc.tensor.matmul_mx(
                    out=y_banks[c][:],
                    lhsT=codes[:].bitcast(FP8X4),
                    lhsT_scale=scales[:],
                    rhs=vw[:, g * DV : (g + 1) * DV].bitcast(FP8X4),
                    rhs_scale=vsc[:, g * DV : (g + 1) * DV],
                    start=(g == pages[0]),
                    stop=(g == pages[-1]),
                )

        y_sb = sb.tile([P, HALVES, DV], F32, name="y_sb")
        out_view = out[0].rearrange("(p c) e -> p c e", c=HALVES)
        for c in range(HALVES):
            nc.scalar.activation(y_sb[:, c, :], y_banks[c][:], ACT.Copy, scale=inv[:, c : c + 1])
            nc.sync.dma_start(out_view[:, c, :], y_sb[:, c, :])
